import numpy as np
import ml_dtypes


def mxq(x, axis, fmt="e4m3"):
    dtype, down = {"e4m3": (ml_dtypes.float8_e4m3fn, 7), "e5m2": (ml_dtypes.float8_e5m2, 14)}[fmt]
    v = np.moveaxis(np.asarray(x, np.float32).astype(ml_dtypes.bfloat16).astype(np.float64), axis, -1)
    blocks = v.reshape(v.shape[:-1] + (-1, 32))
    amax = np.abs(blocks).max(-1, keepdims=True)
    byte = np.maximum(np.where(amax > 0, np.frexp(amax)[1] - 1 + 127, 0) - down, 1)
    scale = np.exp2(byte - 127.0)
    codes = (blocks / scale).astype(np.float32).astype(dtype).astype(np.float64)
    return np.moveaxis((codes * scale).reshape(v.shape), -1, axis)


WIDE = False


def mx_kscale(k):
    if not WIDE:
        return np.ones(k)
    levels = np.array([10, -10, 5, -5, 0])
    if k % 512:
        return np.exp2(np.random.permutation(np.resize(levels, k // 32))).repeat(32)
    a = np.empty((k // 512, 16))
    for p in range(k // 512):
        a[p, :8] = np.random.permutation(np.resize(levels, 8))
        for g in range(8):
            far = levels[np.abs(levels - a[p, g]) >= 10]
            a[p, g + 8] = far[np.random.randint(len(far))]
    return np.exp2(a.ravel()).repeat(32)


def f64(x):
    return np.asarray(x).astype(np.float64)


def striped8(idx):
    return np.concatenate([x.reshape(-1, 16).T for x in idx]).astype(np.uint16)


def runs(offs, k):
    lists = np.stack([offs[16 * r : 16 * r + 16].T.reshape(-1) for r in range(8)]).astype(np.int64)
    return lists[np.arange(k) % 512 // 64]


def pack_weight(w):
    k, n = w.shape
    w = f64(np.asarray(w, np.float32).astype(ml_dtypes.bfloat16)).reshape(k // 32, 32, n)
    amax = np.abs(w).max(1)
    byte = np.clip(np.where(amax > 0, np.frexp(amax)[1] - 1 + 127 - 7, 1), 1, 254)
    scaled = (w * np.exp2(127.0 - byte)[:, None, :]).reshape(k, n).astype(np.float32)
    words = np.ascontiguousarray(scaled.reshape(k // 512, 128, 4, n).transpose(0, 1, 3, 2)).astype(ml_dtypes.float8_e4m3fn).view(np.uint8)
    return words, np.ascontiguousarray(byte.astype(np.uint8).reshape(k // 512, 16, n))


def unpack_weight(words, scales):
    g, p, n, _ = words.shape
    vals = np.ascontiguousarray(words).view(ml_dtypes.float8_e4m3fn).astype(np.float64) * np.repeat(np.exp2(scales.astype(np.float64) - 127.0), 8, axis=1)[..., None]
    return vals.transpose(0, 1, 3, 2).reshape(g * 512, n)

def planes(y):
    n, m = y.shape
    v = y.astype(np.float32).astype(ml_dtypes.bfloat16).astype(np.float64).reshape(n // 32, 32, m)
    top = np.abs(v).max(1)
    byte = np.clip(np.where(top > 0, np.frexp(top)[1] - 1 + 127 - 7, 1), 1, 254)
    codes = (v * np.exp2(127.0 - byte)[:, None, :]).reshape(n, m).astype(np.float32).astype(ml_dtypes.float8_e4m3fn).view(np.uint8)
    words = codes.reshape(n // 512, 128, 4, m).transpose(0, 1, 3, 2)
    return np.ascontiguousarray(words), np.ascontiguousarray(byte.astype(np.uint8).reshape(n // 512, 16, m))


K, T, S, N = 512, 2048, 512, 512


def setup_inputs():
    n = np.random.standard_normal
    s = mx_kscale(K)[:, None]
    packed_xT = pack_weight(n((K, T)) * s)
    return {
        "x_words": packed_xT[0],
        "x_scales": packed_xT[1],
        "w1": (n((K, N)) / np.sqrt(K) / s).astype(np.float32),
        "res": n((N, S)).astype(np.float32),
        "gate": np.random.uniform(0.3, 1.2, (N, 1)).astype(np.float32),
        "offs": striped8(np.stack([np.random.permutation(T)[:S] for _ in range(8)])),
    }


def reference(x_words, x_scales, w1, res, gate, offs):
    xq = unpack_weight(x_words, x_scales)[np.arange(K)[:, None], runs(offs, K)]
    out_0 = f64(res) + f64(gate) * ((mxq(f64(w1), 0, "e4m3").T @ xq))
    return (out_0,) + planes(out_0)

@@ -1,0 +1,142 @@
+from contextlib import ExitStack
+
+import concourse.mybir as mybir
+
+K, T, S, N = 512, 2048, 512, 512
+FLOPS = 2 * K * N * S
+
+F32 = mybir.dt.float32
+BF16 = mybir.dt.bfloat16
+I32 = mybir.dt.int32
+U32 = mybir.dt.uint32
+U16 = mybir.dt.uint16
+U8 = mybir.dt.uint8
+FP8X4 = mybir.dt.float8_e4m3fn_x4
+MULT = mybir.AluOpType.mult
+ADD = mybir.AluOpType.add
+
+P = 128
+PACK = 4
+HALF = S // 2
+W_HALF = N // 2
+SCALAR_TAIL = 128
+
+
+def tile_picked_phout_none_po_kernel(
+    tc, x_words, x_scales, w1, res, gate, offs, out_0, out_1, out_2
+):
+    nc = tc.nc
+    with ExitStack() as ctx:
+        sb = ctx.enter_context(tc.tile_pool(name="sb", bufs=1))
+        ps = ctx.enter_context(tc.psum_pool(name="ps", bufs=1))
+
+        offsets = sb.tile([P, S // 16], U16, name="offsets")
+        nc.sync.dma_start(offsets[:], offs)
+
+        scale_table = sb.tile([P, T], U8, name="scale_table", align_bytes=64)
+        nc.vector.memset(scale_table[:].bitcast(I32), 0)
+        x_plane = sb.tile([P, S], U8, name="x_plane", align_bytes=64)
+        nc.vector.memset(x_plane[:].bitcast(I32), 0)
+
+        gate_sb = sb.tile([P, PACK], F32, name="gate_sb")
+        nc.scalar.dma_start(gate_sb[:], gate.rearrange("(p t) o -> p (t o)", t=PACK))
+        nc.scalar.dma_start(scale_table[:].bitcast(I32)[0:P:8, :], x_scales[0].bitcast(I32))
+
+        w_rows = w1.rearrange("(p j) n -> p j n", j=PACK)
+        w_raw = []
+        for h in range(2):
+            piece = sb.tile([P, PACK, W_HALF], F32, name="w_raw%d" % h, align_bytes=64)
+            nc.sync.dma_start(piece[:], w_rows[:, :, h * W_HALF : (h + 1) * W_HALF])
+            w_raw.append(piece)
+
+        word_table = sb.tile([P, T], I32, name="word_table", align_bytes=64)
+        nc.sync.dma_start(word_table[:], x_words[0].rearrange("p c r -> p (c r)").bitcast(I32))
+
+        res_rows = res.rearrange("(p t) s -> p t s", t=PACK)
+        res_sb = []
+        for c in range(2):
+            piece = sb.tile([P, PACK, HALF], F32, name="res_sb%d" % c, align_bytes=64)
+            nc.sync.dma_start(piece[:], res_rows[:, :, c * HALF : (c + 1) * HALF])
+            res_sb.append(piece)
+
+        picked_scales = sb.tile([P, S], U8, name="picked_scales", align_bytes=64)
+        nc.vector.tensor_copy(picked_scales[:], scale_table[:].indirect(offsets[:]))
+
+        w_bf = sb.tile([P, PACK, P, PACK], BF16, name="w_bf", align_bytes=64)
+
+        def round_w(engine_copy, h):
+            m0 = h * W_HALF // PACK
+            dst = w_bf[:, :, m0 : m0 + W_HALF // PACK, :].rearrange("p (a b) m j -> p a m j b", b=2)
+            src = w_raw[h][:].rearrange("p j (m a b) -> p a m j b", a=2, b=2)
+            engine_copy(dst, src)
+
+        round_w(nc.scalar.copy, 0)
+        for a in range(4):
+            nc.scalar.dma_start(
+                x_plane[:].bitcast(I32)[a:P:32, :], picked_scales[:].bitcast(I32)[8 * a : P : 32, :]
+            )
+        round_w(nc.vector.tensor_copy, 1)
+
+        w_codes = sb.tile([P, N], U32, name="w_codes", align_bytes=64)
+        w_plane = sb.tile([P, N], U8, name="w_plane", align_bytes=64)
+        nc.vector.quantize_mx(
+            out=w_codes[:].bitcast(FP8X4), scales=w_plane[:], in_=w_bf[:].rearrange("p t m j -> p (t m j)")
+        )
+
+        picked_words = []
+        for c in range(2):
+            piece = sb.tile([P, HALF], U32, name="picked_words%d" % c, align_bytes=64)
+            cols = slice(c * HALF // 16, (c + 1) * HALF // 16)
+            nc.vector.tensor_copy(piece[:], word_table[:].bitcast(U32).indirect(offsets[:, cols]))
+            picked_words.append(piece)
+
+        out_rows = out_0.rearrange("(p t) s -> p t s", t=PACK)
+        out_words = out_1[0].rearrange("p c r -> p (c r)").bitcast(I32)
+        y_plane = sb.tile([P, S], U8, name="y_plane", align_bytes=64)
+        y = []
+        for c in range(2):
+            cols = slice(c * HALF, (c + 1) * HALF)
+            y_c = sb.tile([P, PACK, HALF], F32, name="y%d" % c, align_bytes=64)
+            for t in range(PACK):
+                acc = ps.tile([P, HALF], F32, name="acc%d%d" % (c, t))
+                nc.tensor.matmul_mx(
+                    out=acc[:],
+                    lhsT=w_codes[:, t * P : (t + 1) * P].bitcast(FP8X4),
+                    lhsT_scale=w_plane[:, t * P : (t + 1) * P],
+                    rhs=picked_words[c][:].bitcast(FP8X4),
+                    rhs_scale=x_plane[:, cols],
+                    start=True,
+                    stop=True,
+                )
+                nc.vector.scalar_tensor_tensor(
+                    y_c[:, t, :], acc[:], gate_sb[:, t : t + 1], res_sb[c][:, t, :], MULT, ADD
+                )
+            nc.sync.dma_start(out_rows[:, :, cols], y_c[:])
+            y.append(y_c)
+
+        y_bf = [sb.tile([P, HALF, PACK], BF16, name="y_bf%d" % c, align_bytes=64) for c in range(2)]
+
+        def round_y(engine_copy, c, lo, hi):
+            dst = y_bf[c][:, lo:hi, :].rearrange("p (s i) t -> p s t i", i=2)
+            src = y[c][:, :, lo:hi].rearrange("p t (s i) -> p s t i", i=2)
+            engine_copy(dst, src)
+
+        def quantise_y(c):
+            cols = slice(c * HALF, (c + 1) * HALF)
+            codes = sb.tile([P, HALF], I32, name="y_codes%d" % c, align_bytes=64)
+            nc.vector.quantize_mx(
+                out=codes[:].bitcast(FP8X4), scales=y_plane[:, cols], in_=y_bf[c][:].rearrange("p s t -> p (s t)")
+            )
+            nc.sync.dma_start(out_words[:, cols], codes[:])
+
+        round_y(nc.scalar.copy, 0, 0, HALF)
+        round_y(nc.scalar.copy, 1, 0, SCALAR_TAIL)
+        quantise_y(0)
+        round_y(nc.vector.tensor_copy, 1, SCALAR_TAIL, HALF)
+        quantise_y(1)
+
+        for q in range(4):
+            queue = nc.scalar if q % 2 == 0 else nc.sync
+            queue.dma_start(
+                out_2[0].bitcast(I32)[4 * q : 4 * q + 4, :], y_plane[:].bitcast(I32)[32 * q : 32 * q + 4, :]
+            )

@@ -18,7 +18,6 @@ ADD = mybir.AluOpType.add
 P = 128
 PACK = 4
 HALF = S // 2
-W_HALF = N // 2
 SCALAR_TAIL = 128
 
 
@@ -33,55 +32,55 @@ def tile_picked_phout_none_po_kernel(
         offsets = sb.tile([P, S // 16], U16, name="offsets")
         nc.sync.dma_start(offsets[:], offs)
 
-        scale_table = sb.tile([P, T], U8, name="scale_table", align_bytes=64)
+        scale_table = sb.tile([P, T], U8, name="scale_table", tag="scales_then_res", align_bytes=64)
         nc.vector.memset(scale_table[:].bitcast(I32), 0)
         x_plane = sb.tile([P, S], U8, name="x_plane", align_bytes=64)
         nc.vector.memset(x_plane[:].bitcast(I32), 0)
 
-        gate_sb = sb.tile([P, PACK], F32, name="gate_sb")
-        nc.scalar.dma_start(gate_sb[:], gate.rearrange("(p t) o -> p (t o)", t=PACK))
-        nc.scalar.dma_start(scale_table[:].bitcast(I32)[0:P:8, :], x_scales[0].bitcast(I32))
-
         w_rows = w1.rearrange("(p j) n -> p j n", j=PACK)
-        w_raw = []
-        for h in range(2):
-            piece = sb.tile([P, PACK, W_HALF], F32, name="w_raw%d" % h, align_bytes=64)
-            nc.sync.dma_start(piece[:], w_rows[:, :, h * W_HALF : (h + 1) * W_HALF])
-            w_raw.append(piece)
+        w_raw = sb.tile([P, PACK, N], F32, name="w_raw", tag="w_then_res", align_bytes=64)
+        nc.sync.dma_start(w_raw[:, 0:1, :], w_rows[:, 0:1, :])
+        nc.sync.dma_start(scale_table[:].bitcast(I32)[0:P:8, :], x_scales[0].bitcast(I32))
+        nc.sync.dma_start(w_raw[:, 1:PACK, :], w_rows[:, 1:PACK, :])
 
         word_table = sb.tile([P, T], I32, name="word_table", align_bytes=64)
         nc.sync.dma_start(word_table[:], x_words[0].rearrange("p c r -> p (c r)").bitcast(I32))
 
-        res_rows = res.rearrange("(p t) s -> p t s", t=PACK)
-        res_sb = []
-        for c in range(2):
-            piece = sb.tile([P, PACK, HALF], F32, name="res_sb%d" % c, align_bytes=64)
-            nc.sync.dma_start(piece[:], res_rows[:, :, c * HALF : (c + 1) * HALF])
-            res_sb.append(piece)
+        gate_sb = sb.tile([P, PACK], F32, name="gate_sb")
+        nc.sync.dma_start(gate_sb[:], gate.rearrange("(p t) o -> p (t o)", t=PACK))
 
         picked_scales = sb.tile([P, S], U8, name="picked_scales", align_bytes=64)
         nc.vector.tensor_copy(picked_scales[:], scale_table[:].indirect(offsets[:]))
 
-        w_bf = sb.tile([P, PACK, P, PACK], BF16, name="w_bf", align_bytes=64)
-
-        def round_w(engine_copy, h):
-            m0 = h * W_HALF // PACK
-            dst = w_bf[:, :, m0 : m0 + W_HALF // PACK, :].rearrange("p (a b) m j -> p a m j b", b=2)
-            src = w_raw[h][:].rearrange("p j (m a b) -> p a m j b", a=2, b=2)
-            engine_copy(dst, src)
-
-        round_w(nc.scalar.copy, 0)
         for a in range(4):
-            nc.scalar.dma_start(
+            nc.sync.dma_start(
                 x_plane[:].bitcast(I32)[a:P:32, :], picked_scales[:].bitcast(I32)[8 * a : P : 32, :]
             )
-        round_w(nc.vector.tensor_copy, 1)
+
+        w_bf = sb.tile([P, PACK, P, PACK], BF16, name="w_bf", align_bytes=64)
+
+        for a in range(2):
+            nc.vector.tensor_copy(
+                w_bf[:, 2 * a : 2 * a + 2, :, :].rearrange("p b m j -> p m j b"),
+                w_raw[:].rearrange("p j (m t) -> p m j t", t=PACK)[:, :, :, 2 * a : 2 * a + 2],
+            )
+
+        res_rows = res.rearrange("(p t) s -> p t s", t=PACK)
+        res_sb = []
+        for c, tag in enumerate(("scales_then_res", "w_then_res")):
+            piece = sb.tile([P, PACK, HALF], F32, name="res_sb%d" % c, tag=tag, align_bytes=64)
+            nc.sync.dma_start(piece[:], res_rows[:, :, c * HALF : (c + 1) * HALF])
+            res_sb.append(piece)
 
         w_codes = sb.tile([P, N], U32, name="w_codes", align_bytes=64)
         w_plane = sb.tile([P, N], U8, name="w_plane", align_bytes=64)
-        nc.vector.quantize_mx(
-            out=w_codes[:].bitcast(FP8X4), scales=w_plane[:], in_=w_bf[:].rearrange("p t m j -> p (t m j)")
-        )
+        for a in range(2):
+            cols = slice(a * 2 * P, (a + 1) * 2 * P)
+            nc.vector.quantize_mx(
+                out=w_codes[:, cols].bitcast(FP8X4),
+                scales=w_plane[:, cols],
+                in_=w_bf[:, 2 * a : 2 * a + 2, :, :].rearrange("p t m j -> p (t m j)"),
+            )
 
         picked_words = []
         for c in range(2):
@@ -111,7 +110,8 @@ def tile_picked_phout_none_po_kernel(
                 nc.vector.scalar_tensor_tensor(
                     y_c[:, t, :], acc[:], gate_sb[:, t : t + 1], res_sb[c][:, t, :], MULT, ADD
                 )
-            nc.sync.dma_start(out_rows[:, :, cols], y_c[:])
+                if t % 2 == 1:
+                    nc.sync.dma_start(out_rows[:, t - 1 : t + 1, cols], y_c[:, t - 1 : t + 1, :])
             y.append(y_c)
 
         y_bf = [sb.tile([P, HALF, PACK], BF16, name="y_bf%d" % c, align_bytes=64) for c in range(2)]
@@ -131,8 +131,8 @@ def tile_picked_phout_none_po_kernel(
 
         round_y(nc.scalar.copy, 0, 0, HALF)
         round_y(nc.scalar.copy, 1, 0, SCALAR_TAIL)
-        quantise_y(0)
         round_y(nc.vector.tensor_copy, 1, SCALAR_TAIL, HALF)
+        quantise_y(0)
         quantise_y(1)
 
         for q in range(4):

@@ -18,7 +18,8 @@ ADD = mybir.AluOpType.add
 P = 128
 PACK = 4
 HALF = S // 2
-SCALAR_TAIL = 128
+SCALAR_TAIL = 96
+SCALAR_W = 40
 
 
 def tile_picked_phout_none_po_kernel(
@@ -29,9 +30,6 @@ def tile_picked_phout_none_po_kernel(
         sb = ctx.enter_context(tc.tile_pool(name="sb", bufs=1))
         ps = ctx.enter_context(tc.psum_pool(name="ps", bufs=1))
 
-        offsets = sb.tile([P, S // 16], U16, name="offsets")
-        nc.sync.dma_start(offsets[:], offs)
-
         scale_table = sb.tile([P, T], U8, name="scale_table", tag="scales_then_res", align_bytes=64)
         nc.vector.memset(scale_table[:].bitcast(I32), 0)
         x_plane = sb.tile([P, S], U8, name="x_plane", align_bytes=64)
@@ -40,6 +38,8 @@ def tile_picked_phout_none_po_kernel(
         w_rows = w1.rearrange("(p j) n -> p j n", j=PACK)
         w_raw = sb.tile([P, PACK, N], F32, name="w_raw", tag="w_then_res", align_bytes=64)
         nc.sync.dma_start(w_raw[:, 0:1, :], w_rows[:, 0:1, :])
+        offsets = sb.tile([P, S // 16], U16, name="offsets")
+        nc.sync.dma_start(offsets[:], offs)
         nc.sync.dma_start(scale_table[:].bitcast(I32)[0:P:8, :], x_scales[0].bitcast(I32))
         nc.sync.dma_start(w_raw[:, 1:PACK, :], w_rows[:, 1:PACK, :])
 
@@ -47,7 +47,7 @@ def tile_picked_phout_none_po_kernel(
         nc.sync.dma_start(word_table[:], x_words[0].rearrange("p c r -> p (c r)").bitcast(I32))
 
         gate_sb = sb.tile([P, PACK], F32, name="gate_sb")
-        nc.sync.dma_start(gate_sb[:], gate.rearrange("(p t) o -> p (t o)", t=PACK))
+        nc.scalar.dma_start(gate_sb[:], gate.rearrange("(p t) o -> p (t o)", t=PACK))
 
         picked_scales = sb.tile([P, S], U8, name="picked_scales", align_bytes=64)
         nc.vector.tensor_copy(picked_scales[:], scale_table[:].indirect(offsets[:]))
@@ -59,11 +59,18 @@ def tile_picked_phout_none_po_kernel(
 
         w_bf = sb.tile([P, PACK, P, PACK], BF16, name="w_bf", align_bytes=64)
 
-        for a in range(2):
-            nc.vector.tensor_copy(
-                w_bf[:, 2 * a : 2 * a + 2, :, :].rearrange("p b m j -> p m j b"),
-                w_raw[:].rearrange("p j (m t) -> p m j t", t=PACK)[:, :, :, 2 * a : 2 * a + 2],
+        warm = sb.tile([P, 8], F32, name="warm")
+        nc.scalar.copy(warm[:, 0:1], gate_sb[:, 0:1])
+
+        def round_w(engine_copy, a, lo, hi):
+            engine_copy(
+                w_bf[:, 2 * a : 2 * a + 2, lo:hi, :].rearrange("p b m j -> p m j b"),
+                w_raw[:].rearrange("p j (m t) -> p m j t", t=PACK)[:, lo:hi, :, 2 * a : 2 * a + 2],
             )
+
+        for a in range(2):
+            round_w(nc.scalar.copy, a, 0, SCALAR_W)
+            round_w(nc.vector.tensor_copy, a, SCALAR_W, P)
 
         res_rows = res.rearrange("(p t) s -> p t s", t=PACK)
         res_sb = []

@@ -18,7 +18,7 @@ ADD = mybir.AluOpType.add
 P = 128
 PACK = 4
 HALF = S // 2
-SCALAR_TAIL = 96
+QUARTER = S // 4
 SCALAR_W = 40
 
 
@@ -99,48 +99,63 @@ def tile_picked_phout_none_po_kernel(
         out_rows = out_0.rearrange("(p t) s -> p t s", t=PACK)
         out_words = out_1[0].rearrange("p c r -> p (c r)").bitcast(I32)
         y_plane = sb.tile([P, S], U8, name="y_plane", align_bytes=64)
-        y = []
+        y = [sb.tile([P, PACK, HALF], F32, name="y%d" % c, align_bytes=64) for c in range(2)]
+        acc = {}
         for c in range(2):
-            cols = slice(c * HALF, (c + 1) * HALF)
-            y_c = sb.tile([P, PACK, HALF], F32, name="y%d" % c, align_bytes=64)
             for t in range(PACK):
-                acc = ps.tile([P, HALF], F32, name="acc%d%d" % (c, t))
+                acc[c, t] = ps.tile([P, HALF], F32, name="acc%d%d" % (c, t))
                 nc.tensor.matmul_mx(
-                    out=acc[:],
+                    out=acc[c, t][:],
                     lhsT=w_codes[:, t * P : (t + 1) * P].bitcast(FP8X4),
                     lhsT_scale=w_plane[:, t * P : (t + 1) * P],
                     rhs=picked_words[c][:].bitcast(FP8X4),
-                    rhs_scale=x_plane[:, cols],
+                    rhs_scale=x_plane[:, c * HALF : (c + 1) * HALF],
                     start=True,
                     stop=True,
                 )
-                nc.vector.scalar_tensor_tensor(
-                    y_c[:, t, :], acc[:], gate_sb[:, t : t + 1], res_sb[c][:, t, :], MULT, ADD
-                )
-                if t % 2 == 1:
-                    nc.sync.dma_start(out_rows[:, t - 1 : t + 1, cols], y_c[:, t - 1 : t + 1, :])
-            y.append(y_c)
 
-        y_bf = [sb.tile([P, HALF, PACK], BF16, name="y_bf%d" % c, align_bytes=64) for c in range(2)]
+        def finish(c, t, lo, hi):
+            nc.vector.scalar_tensor_tensor(
+                y[c][:, t, lo:hi], acc[c, t][:, lo:hi], gate_sb[:, t : t + 1], res_sb[c][:, t, lo:hi], MULT, ADD
+            )
+
+        def store_y(c, t, rows):
+            nc.sync.dma_start(out_rows[:, t : t + rows, c * HALF : (c + 1) * HALF], y[c][:, t : t + rows, :])
+
+        for t in range(PACK):
+            finish(0, t, 0, HALF)
+            store_y(0, t, 1)
+        finish(1, 0, 0, HALF)
+        finish(1, 1, 0, HALF)
+        store_y(1, 0, 2)
+        finish(1, 2, 0, HALF)
+        finish(1, 3, 0, QUARTER)
+        finish(1, 3, QUARTER, HALF)
+        store_y(1, 2, 2)
 
         def round_y(engine_copy, c, lo, hi):
-            dst = y_bf[c][:, lo:hi, :].rearrange("p (s i) t -> p s t i", i=2)
-            src = y[c][:, :, lo:hi].rearrange("p t (s i) -> p s t i", i=2)
-            engine_copy(dst, src)
-
-        def quantise_y(c):
-            cols = slice(c * HALF, (c + 1) * HALF)
-            codes = sb.tile([P, HALF], I32, name="y_codes%d" % c, align_bytes=64)
-            nc.vector.quantize_mx(
-                out=codes[:].bitcast(FP8X4), scales=y_plane[:, cols], in_=y_bf[c][:].rearrange("p s t -> p (s t)")
+            rounded = sb.tile([P, hi - lo, PACK], BF16, name="y_bf%d_%d" % (c, lo), align_bytes=64)
+            engine_copy(
+                rounded[:].rearrange("p (s i) t -> p s t i", i=2),
+                y[c][:, :, lo:hi].rearrange("p t (s i) -> p s t i", i=2),
             )
-            nc.sync.dma_start(out_words[:, cols], codes[:])
+            return rounded
 
-        round_y(nc.scalar.copy, 0, 0, HALF)
-        round_y(nc.scalar.copy, 1, 0, SCALAR_TAIL)
-        round_y(nc.vector.tensor_copy, 1, SCALAR_TAIL, HALF)
-        quantise_y(0)
-        quantise_y(1)
+        def quantise_y(rounded, codes, lo, hi):
+            nc.vector.quantize_mx(
+                out=codes.bitcast(FP8X4), scales=y_plane[:, lo:hi], in_=rounded[:].rearrange("p s t -> p (s t)")
+            )
+
+        first_half = round_y(nc.scalar.copy, 0, 0, HALF)
+        third_quarter = round_y(nc.vector.tensor_copy, 1, 0, QUARTER)
+        last_quarter = round_y(nc.scalar.copy, 1, QUARTER, HALF)
+
+        codes = [sb.tile([P, HALF], I32, name="y_codes%d" % c, align_bytes=64) for c in range(2)]
+        quantise_y(first_half, codes[0][:], 0, HALF)
+        nc.sync.dma_start(out_words[:, 0:HALF], codes[0][:])
+        quantise_y(third_quarter, codes[1][:, 0:QUARTER], HALF, S - QUARTER)
+        quantise_y(last_quarter, codes[1][:, QUARTER:HALF], S - QUARTER, S)
+        nc.sync.dma_start(out_words[:, HALF:S], codes[1][:])
 
         for q in range(4):
             queue = nc.scalar if q % 2 == 0 else nc.sync

@@ -19,7 +19,8 @@ P = 128
 PACK = 4
 HALF = S // 2
 QUARTER = S // 4
-SCALAR_W = 40
+W_FIRST = 32
+SCALAR_W = 32
 
 
 def tile_picked_phout_none_po_kernel(
@@ -36,12 +37,13 @@ def tile_picked_phout_none_po_kernel(
         nc.vector.memset(x_plane[:].bitcast(I32), 0)
 
         w_rows = w1.rearrange("(p j) n -> p j n", j=PACK)
-        w_raw = sb.tile([P, PACK, N], F32, name="w_raw", tag="w_then_res", align_bytes=64)
-        nc.sync.dma_start(w_raw[:, 0:1, :], w_rows[:, 0:1, :])
+        w_first = sb.tile([P, PACK, W_FIRST * PACK], F32, name="w_first", align_bytes=64)
+        w_rest = sb.tile([P, PACK, N - W_FIRST * PACK], F32, name="w_rest", tag="w_then_res", align_bytes=64)
+        nc.sync.dma_start(w_first[:], w_rows[:, :, 0 : W_FIRST * PACK])
         offsets = sb.tile([P, S // 16], U16, name="offsets")
         nc.sync.dma_start(offsets[:], offs)
         nc.sync.dma_start(scale_table[:].bitcast(I32)[0:P:8, :], x_scales[0].bitcast(I32))
-        nc.sync.dma_start(w_raw[:, 1:PACK, :], w_rows[:, 1:PACK, :])
+        nc.sync.dma_start(w_rest[:], w_rows[:, :, W_FIRST * PACK : N])
 
         word_table = sb.tile([P, T], I32, name="word_table", align_bytes=64)
         nc.sync.dma_start(word_table[:], x_words[0].rearrange("p c r -> p (c r)").bitcast(I32))
@@ -59,18 +61,17 @@ def tile_picked_phout_none_po_kernel(
 
         w_bf = sb.tile([P, PACK, P, PACK], BF16, name="w_bf", align_bytes=64)
 
-        warm = sb.tile([P, 8], F32, name="warm")
-        nc.scalar.copy(warm[:, 0:1], gate_sb[:, 0:1])
-
-        def round_w(engine_copy, a, lo, hi):
+        def round_w(engine_copy, raw, first, a, lo, hi):
             engine_copy(
                 w_bf[:, 2 * a : 2 * a + 2, lo:hi, :].rearrange("p b m j -> p m j b"),
-                w_raw[:].rearrange("p j (m t) -> p m j t", t=PACK)[:, lo:hi, :, 2 * a : 2 * a + 2],
+                raw[:].rearrange("p j (m t) -> p m j t", t=PACK)[:, lo - first : hi - first, :, 2 * a : 2 * a + 2],
             )
 
         for a in range(2):
-            round_w(nc.scalar.copy, a, 0, SCALAR_W)
-            round_w(nc.vector.tensor_copy, a, SCALAR_W, P)
+            round_w(nc.scalar.copy, w_first, 0, a, 0, W_FIRST)
+        for a in range(2):
+            round_w(nc.scalar.copy, w_rest, W_FIRST, a, W_FIRST, W_FIRST + SCALAR_W)
+            round_w(nc.vector.tensor_copy, w_rest, W_FIRST, a, W_FIRST + SCALAR_W, P)
 
         res_rows = res.rearrange("(p t) s -> p t s", t=PACK)
         res_sb = []
@@ -150,7 +151,10 @@ def tile_picked_phout_none_po_kernel(
         third_quarter = round_y(nc.vector.tensor_copy, 1, 0, QUARTER)
         last_quarter = round_y(nc.scalar.copy, 1, QUARTER, HALF)
 
-        codes = [sb.tile([P, HALF], I32, name="y_codes%d" % c, align_bytes=64) for c in range(2)]
+        codes = [
+            sb.tile([P, HALF], I32, name="y_codes%d" % c, tag=tag, align_bytes=64)
+            for c, tag in enumerate(("w_then_res", "late_codes"))
+        ]
         quantise_y(first_half, codes[0][:], 0, HALF)
         nc.sync.dma_start(out_words[:, 0:HALF], codes[0][:])
         quantise_y(third_quarter, codes[1][:, 0:QUARTER], HALF, S - QUARTER)

@@ -19,8 +19,8 @@ P = 128
 PACK = 4
 HALF = S // 2
 QUARTER = S // 4
-W_FIRST = 32
-SCALAR_W = 32
+W_FIRST = 64
+SCALAR_W = 20
 
 
 def tile_picked_phout_none_po_kernel(
@@ -37,7 +37,7 @@ def tile_picked_phout_none_po_kernel(
         nc.vector.memset(x_plane[:].bitcast(I32), 0)
 
         w_rows = w1.rearrange("(p j) n -> p j n", j=PACK)
-        w_first = sb.tile([P, PACK, W_FIRST * PACK], F32, name="w_first", align_bytes=64)
+        w_first = sb.tile([P, PACK, W_FIRST * PACK], F32, name="w_first", tag="w_first_then_res", align_bytes=64)
         w_rest = sb.tile([P, PACK, N - W_FIRST * PACK], F32, name="w_rest", tag="w_then_res", align_bytes=64)
         nc.sync.dma_start(w_first[:], w_rows[:, :, 0 : W_FIRST * PACK])
         offsets = sb.tile([P, S // 16], U16, name="offsets")
@@ -59,7 +59,7 @@ def tile_picked_phout_none_po_kernel(
                 x_plane[:].bitcast(I32)[a:P:32, :], picked_scales[:].bitcast(I32)[8 * a : P : 32, :]
             )
 
-        w_bf = sb.tile([P, PACK, P, PACK], BF16, name="w_bf", align_bytes=64)
+        w_bf = sb.tile([P, PACK, P, PACK], BF16, name="w_bf", tag="w_bf_then_res", align_bytes=64)
 
         def round_w(engine_copy, raw, first, a, lo, hi):
             engine_copy(
@@ -73,13 +73,6 @@ def tile_picked_phout_none_po_kernel(
             round_w(nc.scalar.copy, w_rest, W_FIRST, a, W_FIRST, W_FIRST + SCALAR_W)
             round_w(nc.vector.tensor_copy, w_rest, W_FIRST, a, W_FIRST + SCALAR_W, P)
 
-        res_rows = res.rearrange("(p t) s -> p t s", t=PACK)
-        res_sb = []
-        for c, tag in enumerate(("scales_then_res", "w_then_res")):
-            piece = sb.tile([P, PACK, HALF], F32, name="res_sb%d" % c, tag=tag, align_bytes=64)
-            nc.sync.dma_start(piece[:], res_rows[:, :, c * HALF : (c + 1) * HALF])
-            res_sb.append(piece)
-
         w_codes = sb.tile([P, N], U32, name="w_codes", align_bytes=64)
         w_plane = sb.tile([P, N], U8, name="w_plane", align_bytes=64)
         for a in range(2):
@@ -89,6 +82,18 @@ def tile_picked_phout_none_po_kernel(
                 scales=w_plane[:, cols],
                 in_=w_bf[:, 2 * a : 2 * a + 2, :, :].rearrange("p t m j -> p (t m j)"),
             )
+
+        res_rows = res.rearrange("(p t) s -> p t s", t=PACK)
+        res_sb = {}
+        for c, t, tag in (
+            (0, 0, "scales_then_res"),
+            (0, 2, "w_first_then_res"),
+            (1, 0, "w_then_res"),
+            (1, 2, "w_bf_then_res"),
+        ):
+            piece = sb.tile([P, 2, HALF], F32, name="res_sb%d%d" % (c, t), tag=tag, align_bytes=64)
+            nc.sync.dma_start(piece[:], res_rows[:, t : t + 2, c * HALF : (c + 1) * HALF])
+            res_sb[c, t], res_sb[c, t + 1] = piece[:, 0, :], piece[:, 1, :]
 
         picked_words = []
         for c in range(2):
@@ -117,7 +122,7 @@ def tile_picked_phout_none_po_kernel(
 
         def finish(c, t, lo, hi):
             nc.vector.scalar_tensor_tensor(
-                y[c][:, t, lo:hi], acc[c, t][:, lo:hi], gate_sb[:, t : t + 1], res_sb[c][:, t, lo:hi], MULT, ADD
+                y[c][:, t, lo:hi], acc[c, t][:, lo:hi], gate_sb[:, t : t + 1], res_sb[c, t][:, lo:hi], MULT, ADD
             )
 
         def store_y(c, t, rows):
@@ -125,7 +130,8 @@ def tile_picked_phout_none_po_kernel(
 
         for t in range(PACK):
             finish(0, t, 0, HALF)
-            store_y(0, t, 1)
+            if t % 2 == 1:
+                store_y(0, t - 1, 2)
         finish(1, 0, 0, HALF)
         finish(1, 1, 0, HALF)
         store_y(1, 0, 2)
@@ -153,7 +159,7 @@ def tile_picked_phout_none_po_kernel(
 
         codes = [
             sb.tile([P, HALF], I32, name="y_codes%d" % c, tag=tag, align_bytes=64)
-            for c, tag in enumerate(("w_then_res", "late_codes"))
+            for c, tag in enumerate(("w_bf_then_res", "late_codes"))
         ]
         quantise_y(first_half, codes[0][:], 0, HALF)
         nc.sync.dma_start(out_words[:, 0:HALF], codes[0][:])

@@ -19,8 +19,8 @@ P = 128
 PACK = 4
 HALF = S // 2
 QUARTER = S // 4
-W_FIRST = 64
-SCALAR_W = 20
+W_FIRST = 768
+SCALAR_W = 32
 
 
 def tile_picked_phout_none_po_kernel(
@@ -29,21 +29,21 @@ def tile_picked_phout_none_po_kernel(
     nc = tc.nc
     with ExitStack() as ctx:
         sb = ctx.enter_context(tc.tile_pool(name="sb", bufs=1))
+        shared = ctx.enter_context(tc.tile_pool(name="shared", bufs=1))
         ps = ctx.enter_context(tc.psum_pool(name="ps", bufs=1))
 
-        scale_table = sb.tile([P, T], U8, name="scale_table", tag="scales_then_res", align_bytes=64)
+        scale_table = shared.tile([P, T], U8, name="scale_table", offset=T // 2, align_bytes=64)
         nc.vector.memset(scale_table[:].bitcast(I32), 0)
         x_plane = sb.tile([P, S], U8, name="x_plane", align_bytes=64)
         nc.vector.memset(x_plane[:].bitcast(I32), 0)
 
-        w_rows = w1.rearrange("(p j) n -> p j n", j=PACK)
-        w_first = sb.tile([P, PACK, W_FIRST * PACK], F32, name="w_first", tag="w_first_then_res", align_bytes=64)
-        w_rest = sb.tile([P, PACK, N - W_FIRST * PACK], F32, name="w_rest", tag="w_then_res", align_bytes=64)
-        nc.sync.dma_start(w_first[:], w_rows[:, :, 0 : W_FIRST * PACK])
+        w_rows = w1.rearrange("(p j) n -> p (j n)", j=PACK)
+        w_raw = sb.tile([P, PACK * N], F32, name="w_raw", tag="w_then_res", align_bytes=64)
+        nc.sync.dma_start(w_raw[:, 0:W_FIRST], w_rows[:, 0:W_FIRST])
         offsets = sb.tile([P, S // 16], U16, name="offsets")
         nc.sync.dma_start(offsets[:], offs)
         nc.sync.dma_start(scale_table[:].bitcast(I32)[0:P:8, :], x_scales[0].bitcast(I32))
-        nc.sync.dma_start(w_rest[:], w_rows[:, :, W_FIRST * PACK : N])
+        nc.sync.dma_start(w_raw[:, W_FIRST : PACK * N], w_rows[:, W_FIRST : PACK * N])
 
         word_table = sb.tile([P, T], I32, name="word_table", align_bytes=64)
         nc.sync.dma_start(word_table[:], x_words[0].rearrange("p c r -> p (c r)").bitcast(I32))
@@ -61,17 +61,17 @@ def tile_picked_phout_none_po_kernel(
 
         w_bf = sb.tile([P, PACK, P, PACK], BF16, name="w_bf", tag="w_bf_then_res", align_bytes=64)
 
-        def round_w(engine_copy, raw, first, a, lo, hi):
-            engine_copy(
-                w_bf[:, 2 * a : 2 * a + 2, lo:hi, :].rearrange("p b m j -> p m j b"),
-                raw[:].rearrange("p j (m t) -> p m j t", t=PACK)[:, lo - first : hi - first, :, 2 * a : 2 * a + 2],
+        w_view = w_raw[:].rearrange("p (j m t) -> p j m t", j=PACK, t=PACK)
+        for u in range(2):
+            nc.scalar.copy(
+                w_bf[:, :, 0:SCALAR_W, 2 * u : 2 * u + 2].rearrange("p t (g i) j -> p g t i j", i=2),
+                w_view[:, 2 * u : 2 * u + 2, 0:SCALAR_W, :].rearrange("p j (g i) t -> p g t i j", i=2),
             )
-
         for a in range(2):
-            round_w(nc.scalar.copy, w_first, 0, a, 0, W_FIRST)
-        for a in range(2):
-            round_w(nc.scalar.copy, w_rest, W_FIRST, a, W_FIRST, W_FIRST + SCALAR_W)
-            round_w(nc.vector.tensor_copy, w_rest, W_FIRST, a, W_FIRST + SCALAR_W, P)
+            nc.vector.tensor_copy(
+                w_bf[:, 2 * a : 2 * a + 2, SCALAR_W:P, :].rearrange("p b m j -> p m j b"),
+                w_view[:, :, SCALAR_W:P, 2 * a : 2 * a + 2].rearrange("p j m b -> p m j b"),
+            )
 
         w_codes = sb.tile([P, N], U32, name="w_codes", align_bytes=64)
         w_plane = sb.tile([P, N], U8, name="w_plane", align_bytes=64)
@@ -85,13 +85,14 @@ def tile_picked_phout_none_po_kernel(
 
         res_rows = res.rearrange("(p t) s -> p t s", t=PACK)
         res_sb = {}
-        for c, t, tag in (
-            (0, 0, "scales_then_res"),
-            (0, 2, "w_first_then_res"),
-            (1, 0, "w_then_res"),
-            (1, 2, "w_bf_then_res"),
-        ):
-            piece = sb.tile([P, 2, HALF], F32, name="res_sb%d%d" % (c, t), tag=tag, align_bytes=64)
+        res_pieces = [
+            shared.tile([P, 2, HALF], F32, name="res_sb00", offset=0, align_bytes=64),
+            shared.tile([P, 2, HALF], F32, name="res_sb02", offset=T, align_bytes=64),
+            sb.tile([P, 2, HALF], F32, name="res_sb10", tag="w_then_res", align_bytes=64),
+            sb.tile([P, 2, HALF], F32, name="res_sb12", tag="w_bf_then_res", align_bytes=64),
+        ]
+        for i, piece in enumerate(res_pieces):
+            c, t = i // 2, 2 * (i % 2)
             nc.sync.dma_start(piece[:], res_rows[:, t : t + 2, c * HALF : (c + 1) * HALF])
             res_sb[c, t], res_sb[c, t + 1] = piece[:, 0, :], piece[:, 1, :]
 

@@ -48,6 +48,10 @@ def tile_picked_phout_none_po_kernel(
         word_table = sb.tile([P, T], I32, name="word_table", align_bytes=64)
         nc.sync.dma_start(word_table[:], x_words[0].rearrange("p c r -> p (c r)").bitcast(I32))
 
+        res_rows = res.rearrange("(p t) s -> p t s", t=PACK)
+        res_early = sb.tile([P, 2, HALF], F32, name="res_sb00", align_bytes=64)
+        nc.sync.dma_start(res_early[:], res_rows[:, 0:2, 0:HALF])
+
         gate_sb = sb.tile([P, PACK], F32, name="gate_sb")
         nc.scalar.dma_start(gate_sb[:], gate.rearrange("(p t) o -> p (t o)", t=PACK))
 
@@ -59,7 +63,7 @@ def tile_picked_phout_none_po_kernel(
                 x_plane[:].bitcast(I32)[a:P:32, :], picked_scales[:].bitcast(I32)[8 * a : P : 32, :]
             )
 
-        w_bf = sb.tile([P, PACK, P, PACK], BF16, name="w_bf", tag="w_bf_then_res", align_bytes=64)
+        w_bf = sb.tile([P, PACK, P, PACK], BF16, name="w_bf", align_bytes=64)
 
         w_view = w_raw[:].rearrange("p (j m t) -> p j m t", j=PACK, t=PACK)
         for u in range(2):
@@ -83,15 +87,13 @@ def tile_picked_phout_none_po_kernel(
                 in_=w_bf[:, 2 * a : 2 * a + 2, :, :].rearrange("p t m j -> p (t m j)"),
             )
 
-        res_rows = res.rearrange("(p t) s -> p t s", t=PACK)
-        res_sb = {}
+        res_sb = {(0, 0): res_early[:, 0, :], (0, 1): res_early[:, 1, :]}
         res_pieces = [
-            shared.tile([P, 2, HALF], F32, name="res_sb00", offset=0, align_bytes=64),
-            shared.tile([P, 2, HALF], F32, name="res_sb02", offset=T, align_bytes=64),
-            sb.tile([P, 2, HALF], F32, name="res_sb10", tag="w_then_res", align_bytes=64),
-            sb.tile([P, 2, HALF], F32, name="res_sb12", tag="w_bf_then_res", align_bytes=64),
+            shared.tile([P, 2, HALF], F32, name="res_sb02", offset=0, align_bytes=64),
+            shared.tile([P, 2, HALF], F32, name="res_sb10", offset=T, align_bytes=64),
+            sb.tile([P, 2, HALF], F32, name="res_sb12", tag="w_then_res", align_bytes=64),
         ]
-        for i, piece in enumerate(res_pieces):
+        for i, piece in enumerate(res_pieces, 1):
             c, t = i // 2, 2 * (i % 2)
             nc.sync.dma_start(piece[:], res_rows[:, t : t + 2, c * HALF : (c + 1) * HALF])
             res_sb[c, t], res_sb[c, t + 1] = piece[:, 0, :], piece[:, 1, :]
@@ -160,7 +162,7 @@ def tile_picked_phout_none_po_kernel(
 
         codes = [
             sb.tile([P, HALF], I32, name="y_codes%d" % c, tag=tag, align_bytes=64)
-            for c, tag in enumerate(("w_bf_then_res", "late_codes"))
+            for c, tag in enumerate(("w_then_res", "late_codes"))
         ]
         quantise_y(first_half, codes[0][:], 0, HALF)
         nc.sync.dma_start(out_words[:, 0:HALF], codes[0][:])

@@ -20,7 +20,7 @@ PACK = 4
 HALF = S // 2
 QUARTER = S // 4
 W_FIRST = 768
-SCALAR_W = 32
+SCALAR_W = 64
 
 
 def tile_picked_phout_none_po_kernel(
@@ -66,10 +66,10 @@ def tile_picked_phout_none_po_kernel(
         w_bf = sb.tile([P, PACK, P, PACK], BF16, name="w_bf", align_bytes=64)
 
         w_view = w_raw[:].rearrange("p (j m t) -> p j m t", j=PACK, t=PACK)
-        for u in range(2):
+        for u, tiles in ((0, slice(0, 4)), (1, slice(0, 2)), (1, slice(2, 4))):
             nc.scalar.copy(
-                w_bf[:, :, 0:SCALAR_W, 2 * u : 2 * u + 2].rearrange("p t (g i) j -> p g t i j", i=2),
-                w_view[:, 2 * u : 2 * u + 2, 0:SCALAR_W, :].rearrange("p j (g i) t -> p g t i j", i=2),
+                w_bf[:, tiles, 0:SCALAR_W, 2 * u : 2 * u + 2].rearrange("p t (g i) j -> p g t i j", i=2),
+                w_view[:, 2 * u : 2 * u + 2, 0:SCALAR_W, tiles].rearrange("p j (g i) t -> p g t i j", i=2),
             )
         for a in range(2):
             nc.vector.tensor_copy(

@@ -21,6 +21,7 @@ HALF = S // 2
 QUARTER = S // 4
 W_FIRST = 768
 SCALAR_W = 64
+GPSIMD_Y = 72
 
 
 def tile_picked_phout_none_po_kernel(
@@ -32,10 +33,8 @@ def tile_picked_phout_none_po_kernel(
         shared = ctx.enter_context(tc.tile_pool(name="shared", bufs=1))
         ps = ctx.enter_context(tc.psum_pool(name="ps", bufs=1))
 
-        scale_table = shared.tile([P, T], U8, name="scale_table", offset=T // 2, align_bytes=64)
+        scale_table = sb.tile([P, T], U8, name="scale_table", align_bytes=64)
         nc.vector.memset(scale_table[:].bitcast(I32), 0)
-        x_plane = sb.tile([P, S], U8, name="x_plane", align_bytes=64)
-        nc.vector.memset(x_plane[:].bitcast(I32), 0)
 
         w_rows = w1.rearrange("(p j) n -> p (j n)", j=PACK)
         w_raw = sb.tile([P, PACK * N], F32, name="w_raw", tag="w_then_res", align_bytes=64)
@@ -55,13 +54,13 @@ def tile_picked_phout_none_po_kernel(
         gate_sb = sb.tile([P, PACK], F32, name="gate_sb")
         nc.scalar.dma_start(gate_sb[:], gate.rearrange("(p t) o -> p (t o)", t=PACK))
 
-        picked_scales = sb.tile([P, S], U8, name="picked_scales", align_bytes=64)
+        picked_scales = shared.tile([P, S], U8, name="picked_scales", offset=T - S // 2, align_bytes=64)
         nc.vector.tensor_copy(picked_scales[:], scale_table[:].indirect(offsets[:]))
 
-        for a in range(4):
-            nc.sync.dma_start(
-                x_plane[:].bitcast(I32)[a:P:32, :], picked_scales[:].bitcast(I32)[8 * a : P : 32, :]
-            )
+        x_plane = sb.tile([P, S], U8, name="x_plane", align_bytes=64)
+        nc.vector.tensor_copy(x_plane[:].bitcast(I32), picked_scales[:].bitcast(I32))
+        for a in range(1, 4):
+            nc.sync.dma_start(x_plane[:].bitcast(I32)[a:P:32, :], x_plane[:].bitcast(I32)[8 * a : P : 32, :])
 
         w_bf = sb.tile([P, PACK, P, PACK], BF16, name="w_bf", align_bytes=64)
 
@@ -156,7 +155,15 @@ def tile_picked_phout_none_po_kernel(
                 out=codes.bitcast(FP8X4), scales=y_plane[:, lo:hi], in_=rounded[:].rearrange("p s t -> p (s t)")
             )
 
-        first_half = round_y(nc.scalar.copy, 0, 0, HALF)
+        first_half = sb.tile([P, HALF, PACK], BF16, name="first_half", align_bytes=64)
+        split = HALF - GPSIMD_Y
+        nc.scalar.copy(
+            first_half[:, 0:split, :].rearrange("p (s i) t -> p s t i", i=2),
+            y[0][:, :, 0:split].rearrange("p t (s i) -> p s t i", i=2),
+        )
+        nc.gpsimd.tensor_scalar(
+            first_half[:, split:HALF, :], y[0][:, :, split:HALF].rearrange("p t s -> p s t"), 1.0, 0.0, MULT, ADD
+        )
         third_quarter = round_y(nc.vector.tensor_copy, 1, 0, QUARTER)
         last_quarter = round_y(nc.scalar.copy, 1, QUARTER, HALF)
 

@@ -19,7 +19,7 @@ P = 128
 PACK = 4
 HALF = S // 2
 QUARTER = S // 4
-W_FIRST = 768
+W_FIRST = 1024
 SCALAR_W = 64
 GPSIMD_Y = 72
 
@@ -41,7 +41,9 @@ def tile_picked_phout_none_po_kernel(
         nc.sync.dma_start(w_raw[:, 0:W_FIRST], w_rows[:, 0:W_FIRST])
         offsets = sb.tile([P, S // 16], U16, name="offsets")
         nc.sync.dma_start(offsets[:], offs)
-        nc.sync.dma_start(scale_table[:].bitcast(I32)[0:P:8, :], x_scales[0].bitcast(I32))
+        scale_rows = x_scales[0].bitcast(I32).rearrange("(u e) c -> e u c", e=2)
+        for e in range(2):
+            nc.sync.dma_start(scale_table[:].bitcast(I32)[e:P:16, :], scale_rows[e])
         nc.sync.dma_start(w_raw[:, W_FIRST : PACK * N], w_rows[:, W_FIRST : PACK * N])
 
         word_table = sb.tile([P, T], I32, name="word_table", align_bytes=64)
@@ -52,15 +54,18 @@ def tile_picked_phout_none_po_kernel(
         nc.sync.dma_start(res_early[:], res_rows[:, 0:2, 0:HALF])
 
         gate_sb = sb.tile([P, PACK], F32, name="gate_sb")
-        nc.scalar.dma_start(gate_sb[:], gate.rearrange("(p t) o -> p (t o)", t=PACK))
+        nc.gpsimd.dma_start(gate_sb[:], gate.rearrange("(p t) o -> p (t o)", t=PACK))
 
-        picked_scales = shared.tile([P, S], U8, name="picked_scales", offset=T - S // 2, align_bytes=64)
-        nc.vector.tensor_copy(picked_scales[:], scale_table[:].indirect(offsets[:]))
-
-        x_plane = sb.tile([P, S], U8, name="x_plane", align_bytes=64)
-        nc.vector.tensor_copy(x_plane[:].bitcast(I32), picked_scales[:].bitcast(I32))
-        for a in range(1, 4):
-            nc.sync.dma_start(x_plane[:].bitcast(I32)[a:P:32, :], x_plane[:].bitcast(I32)[8 * a : P : 32, :])
+        x_plane = []
+        for c in range(2):
+            picked = shared.tile([P, HALF], U8, name="picked_scales%d" % c, offset=c * T, align_bytes=64)
+            cols = slice(c * HALF // 16, (c + 1) * HALF // 16)
+            nc.vector.tensor_copy(picked[:], scale_table[:].indirect(offsets[:, cols]))
+            plane = sb.tile([P, HALF], U8, name="x_plane%d" % c, align_bytes=64)
+            nc.vector.tensor_copy(plane[:].bitcast(I32), picked[:].bitcast(I32))
+            for e in range(2):
+                nc.sync.dma_start(plane[:].bitcast(I32)[2 + e : P : 32, :], plane[:].bitcast(I32)[16 + e : P : 32, :])
+            x_plane.append(plane)
 
         w_bf = sb.tile([P, PACK, P, PACK], BF16, name="w_bf", align_bytes=64)
 
@@ -117,7 +122,7 @@ def tile_picked_phout_none_po_kernel(
                     lhsT=w_codes[:, t * P : (t + 1) * P].bitcast(FP8X4),
                     lhsT_scale=w_plane[:, t * P : (t + 1) * P],
                     rhs=picked_words[c][:].bitcast(FP8X4),
-                    rhs_scale=x_plane[:, c * HALF : (c + 1) * HALF],
+                    rhs_scale=x_plane[c][:],
                     start=True,
                     stop=True,
                 )

@@ -37,7 +37,7 @@ def tile_picked_phout_none_po_kernel(
         nc.vector.memset(scale_table[:].bitcast(I32), 0)
 
         w_rows = w1.rearrange("(p j) n -> p (j n)", j=PACK)
-        w_raw = sb.tile([P, PACK * N], F32, name="w_raw", tag="w_then_res", align_bytes=64)
+        w_raw = sb.tile([P, PACK * N], F32, name="w_raw", align_bytes=64)
         nc.sync.dma_start(w_raw[:, 0:W_FIRST], w_rows[:, 0:W_FIRST])
         offsets = sb.tile([P, S // 16], U16, name="offsets")
         nc.sync.dma_start(offsets[:], offs)
@@ -51,14 +51,15 @@ def tile_picked_phout_none_po_kernel(
 
         res_rows = res.rearrange("(p t) s -> p t s", t=PACK)
         res_early = sb.tile([P, 2, HALF], F32, name="res_sb00", align_bytes=64)
-        nc.sync.dma_start(res_early[:], res_rows[:, 0:2, 0:HALF])
+        nc.sync.dma_start(res_early[:], res_rows[:, 2:4, 0:HALF])
 
         gate_sb = sb.tile([P, PACK], F32, name="gate_sb")
         nc.gpsimd.dma_start(gate_sb[:], gate.rearrange("(p t) o -> p (t o)", t=PACK))
 
         x_plane = []
+        res_late = []
         for c in range(2):
-            picked = shared.tile([P, HALF], U8, name="picked_scales%d" % c, offset=c * T, align_bytes=64)
+            picked = shared.tile([P, HALF], U8, name="picked_scales%d" % c, offset=c * 2 * T, align_bytes=64)
             cols = slice(c * HALF // 16, (c + 1) * HALF // 16)
             nc.vector.tensor_copy(picked[:], scale_table[:].indirect(offsets[:, cols]))
             plane = sb.tile([P, HALF], U8, name="x_plane%d" % c, align_bytes=64)
@@ -66,6 +67,10 @@ def tile_picked_phout_none_po_kernel(
             for e in range(2):
                 nc.sync.dma_start(plane[:].bitcast(I32)[2 + e : P : 32, :], plane[:].bitcast(I32)[16 + e : P : 32, :])
             x_plane.append(plane)
+            source = res_rows[:, 0:2, :] if c == 0 else res_rows[:, 2:4, HALF:S]
+            piece = shared.tile(list(source.shape), F32, name="res_late%d" % c, offset=c * 2 * T, align_bytes=64)
+            nc.sync.dma_start(piece[:], source)
+            res_late.append(piece)
 
         w_bf = sb.tile([P, PACK, P, PACK], BF16, name="w_bf", align_bytes=64)
 
@@ -91,16 +96,11 @@ def tile_picked_phout_none_po_kernel(
                 in_=w_bf[:, 2 * a : 2 * a + 2, :, :].rearrange("p t m j -> p (t m j)"),
             )
 
-        res_sb = {(0, 0): res_early[:, 0, :], (0, 1): res_early[:, 1, :]}
-        res_pieces = [
-            shared.tile([P, 2, HALF], F32, name="res_sb02", offset=0, align_bytes=64),
-            shared.tile([P, 2, HALF], F32, name="res_sb10", offset=T, align_bytes=64),
-            sb.tile([P, 2, HALF], F32, name="res_sb12", tag="w_then_res", align_bytes=64),
-        ]
-        for i, piece in enumerate(res_pieces, 1):
-            c, t = i // 2, 2 * (i % 2)
-            nc.sync.dma_start(piece[:], res_rows[:, t : t + 2, c * HALF : (c + 1) * HALF])
-            res_sb[c, t], res_sb[c, t + 1] = piece[:, 0, :], piece[:, 1, :]
+        res_whole, res_last = res_late
+        res_sb = {}
+        for t in range(2):
+            res_sb[0, 2 + t], res_sb[1, 2 + t] = res_early[:, t, :], res_last[:, t, :]
+            res_sb[0, t], res_sb[1, t] = res_whole[:, t, 0:HALF], res_whole[:, t, HALF:S]
 
         picked_words = []
         for c in range(2):
@@ -115,7 +115,7 @@ def tile_picked_phout_none_po_kernel(
         y = [sb.tile([P, PACK, HALF], F32, name="y%d" % c, align_bytes=64) for c in range(2)]
         acc = {}
         for c in range(2):
-            for t in range(PACK):
+            for t in (2, 3, 0, 1) if c == 0 else range(PACK):
                 acc[c, t] = ps.tile([P, HALF], F32, name="acc%d%d" % (c, t))
                 nc.tensor.matmul_mx(
                     out=acc[c, t][:],
@@ -135,13 +135,13 @@ def tile_picked_phout_none_po_kernel(
         def store_y(c, t, rows):
             nc.sync.dma_start(out_rows[:, t : t + rows, c * HALF : (c + 1) * HALF], y[c][:, t : t + rows, :])
 
-        for t in range(PACK):
+        for t in (2, 3):
             finish(0, t, 0, HALF)
-            if t % 2 == 1:
-                store_y(0, t - 1, 2)
-        finish(1, 0, 0, HALF)
-        finish(1, 1, 0, HALF)
-        store_y(1, 0, 2)
+            store_y(0, t, 1)
+        for c in range(2):
+            finish(c, 0, 0, HALF)
+            finish(c, 1, 0, HALF)
+            store_y(c, 0, 2)
         finish(1, 2, 0, HALF)
         finish(1, 3, 0, QUARTER)
         finish(1, 3, QUARTER, HALF)
@@ -173,8 +173,8 @@ def tile_picked_phout_none_po_kernel(
         last_quarter = round_y(nc.scalar.copy, 1, QUARTER, HALF)
 
         codes = [
-            sb.tile([P, HALF], I32, name="y_codes%d" % c, tag=tag, align_bytes=64)
-            for c, tag in enumerate(("w_then_res", "late_codes"))
+            shared.tile([P, HALF], I32, name="y_codes0", offset=2 * T, align_bytes=64),
+            sb.tile([P, HALF], I32, name="y_codes1", align_bytes=64),
         ]
         quantise_y(first_half, codes[0][:], 0, HALF)
         nc.sync.dma_start(out_words[:, 0:HALF], codes[0][:])

@@ -22,6 +22,7 @@ QUARTER = S // 4
 W_FIRST = 1024
 SCALAR_W = 64
 GPSIMD_Y = 72
+VECTOR_Y = 160
 
 
 def tile_picked_phout_none_po_kernel(
@@ -143,21 +144,13 @@ def tile_picked_phout_none_po_kernel(
             finish(c, 1, 0, HALF)
             store_y(c, 0, 2)
         finish(1, 2, 0, HALF)
-        finish(1, 3, 0, QUARTER)
-        finish(1, 3, QUARTER, HALF)
+        finish(1, 3, 0, VECTOR_Y)
+        finish(1, 3, VECTOR_Y, HALF)
         store_y(1, 2, 2)
-
-        def round_y(engine_copy, c, lo, hi):
-            rounded = sb.tile([P, hi - lo, PACK], BF16, name="y_bf%d_%d" % (c, lo), align_bytes=64)
-            engine_copy(
-                rounded[:].rearrange("p (s i) t -> p s t i", i=2),
-                y[c][:, :, lo:hi].rearrange("p t (s i) -> p s t i", i=2),
-            )
-            return rounded
 
         def quantise_y(rounded, codes, lo, hi):
             nc.vector.quantize_mx(
-                out=codes.bitcast(FP8X4), scales=y_plane[:, lo:hi], in_=rounded[:].rearrange("p s t -> p (s t)")
+                out=codes.bitcast(FP8X4), scales=y_plane[:, lo:hi], in_=rounded.rearrange("p s t -> p (s t)")
             )
 
         first_half = sb.tile([P, HALF, PACK], BF16, name="first_half", align_bytes=64)
@@ -169,17 +162,21 @@ def tile_picked_phout_none_po_kernel(
         nc.gpsimd.tensor_scalar(
             first_half[:, split:HALF, :], y[0][:, :, split:HALF].rearrange("p t s -> p s t"), 1.0, 0.0, MULT, ADD
         )
-        third_quarter = round_y(nc.vector.tensor_copy, 1, 0, QUARTER)
-        last_quarter = round_y(nc.scalar.copy, 1, QUARTER, HALF)
+        second_half = sb.tile([P, HALF, PACK], BF16, name="second_half", align_bytes=64)
+        for engine_copy, lo, hi in ((nc.vector.tensor_copy, 0, VECTOR_Y), (nc.scalar.copy, VECTOR_Y, HALF)):
+            engine_copy(
+                second_half[:, lo:hi, :].rearrange("p (s i) t -> p s t i", i=2),
+                y[1][:, :, lo:hi].rearrange("p t (s i) -> p s t i", i=2),
+            )
 
         codes = [
             shared.tile([P, HALF], I32, name="y_codes0", offset=2 * T, align_bytes=64),
             sb.tile([P, HALF], I32, name="y_codes1", align_bytes=64),
         ]
-        quantise_y(first_half, codes[0][:], 0, HALF)
+        quantise_y(first_half[:], codes[0][:], 0, HALF)
         nc.sync.dma_start(out_words[:, 0:HALF], codes[0][:])
-        quantise_y(third_quarter, codes[1][:, 0:QUARTER], HALF, S - QUARTER)
-        quantise_y(last_quarter, codes[1][:, QUARTER:HALF], S - QUARTER, S)
+        quantise_y(second_half[:, 0:QUARTER, :], codes[1][:, 0:QUARTER], HALF, S - QUARTER)
+        quantise_y(second_half[:, QUARTER:HALF, :], codes[1][:, QUARTER:HALF], S - QUARTER, S)
         nc.sync.dma_start(out_words[:, HALF:S], codes[1][:])
 
         for q in range(4):

@@ -38,7 +38,7 @@ def tile_picked_phout_none_po_kernel(
         nc.vector.memset(scale_table[:].bitcast(I32), 0)
 
         w_rows = w1.rearrange("(p j) n -> p (j n)", j=PACK)
-        w_raw = sb.tile([P, PACK * N], F32, name="w_raw", align_bytes=64)
+        w_raw = shared.tile([P, PACK * N], F32, name="w_raw", offset=T, align_bytes=64)
         nc.sync.dma_start(w_raw[:, 0:W_FIRST], w_rows[:, 0:W_FIRST])
         offsets = sb.tile([P, S // 16], U16, name="offsets")
         nc.sync.dma_start(offsets[:], offs)
@@ -54,24 +54,28 @@ def tile_picked_phout_none_po_kernel(
         res_early = sb.tile([P, 2, HALF], F32, name="res_sb00", align_bytes=64)
         nc.sync.dma_start(res_early[:], res_rows[:, 2:4, 0:HALF])
 
+        res_whole = sb.tile([P, 2, S], F32, name="res_whole", align_bytes=64)
+        nc.sync.dma_start(res_whole[:], res_rows[:, 0:2, :])
+        res_last = shared.tile([P, 2, HALF], F32, name="res_last", offset=0, align_bytes=64)
+        nc.sync.dma_start(res_last[:], res_rows[:, 2:4, HALF:S])
+
         gate_sb = sb.tile([P, PACK], F32, name="gate_sb")
         nc.gpsimd.dma_start(gate_sb[:], gate.rearrange("(p t) o -> p (t o)", t=PACK))
 
-        x_plane = []
-        res_late = []
+        picked = []
         for c in range(2):
-            picked = shared.tile([P, HALF], U8, name="picked_scales%d" % c, offset=c * 2 * T, align_bytes=64)
+            piece = sb.tile([P, HALF], U8, name="picked_scales%d" % c, align_bytes=64)
             cols = slice(c * HALF // 16, (c + 1) * HALF // 16)
-            nc.vector.tensor_copy(picked[:], scale_table[:].indirect(offsets[:, cols]))
-            plane = sb.tile([P, HALF], U8, name="x_plane%d" % c, align_bytes=64)
-            nc.vector.tensor_copy(plane[:].bitcast(I32), picked[:].bitcast(I32))
+            nc.vector.tensor_copy(piece[:], scale_table[:].indirect(offsets[:, cols]))
+            picked.append(piece)
+
+        def place_rows(plane, rows):
+            nc.vector.tensor_copy(plane[:].bitcast(I32), rows[:].bitcast(I32))
             for e in range(2):
-                nc.sync.dma_start(plane[:].bitcast(I32)[2 + e : P : 32, :], plane[:].bitcast(I32)[16 + e : P : 32, :])
-            x_plane.append(plane)
-            source = res_rows[:, 0:2, :] if c == 0 else res_rows[:, 2:4, HALF:S]
-            piece = shared.tile(list(source.shape), F32, name="res_late%d" % c, offset=c * 2 * T, align_bytes=64)
-            nc.sync.dma_start(piece[:], source)
-            res_late.append(piece)
+                nc.scalar.dma_start(plane[:].bitcast(I32)[2 + e : P : 32, :], plane[:].bitcast(I32)[16 + e : P : 32, :])
+
+        plane_first = sb.tile([P, HALF], U8, name="x_plane0", align_bytes=64)
+        place_rows(plane_first, picked[0])
 
         w_bf = sb.tile([P, PACK, P, PACK], BF16, name="w_bf", align_bytes=64)
 
@@ -87,6 +91,10 @@ def tile_picked_phout_none_po_kernel(
                 w_view[:, :, SCALAR_W:P, 2 * a : 2 * a + 2].rearrange("p j m b -> p m j b"),
             )
 
+        plane_second = shared.tile([P, HALF], U8, name="x_plane1", offset=T, align_bytes=64)
+        place_rows(plane_second, picked[1])
+        x_plane = [plane_first, plane_second]
+
         w_codes = sb.tile([P, N], U32, name="w_codes", align_bytes=64)
         w_plane = sb.tile([P, N], U8, name="w_plane", align_bytes=64)
         for a in range(2):
@@ -97,7 +105,6 @@ def tile_picked_phout_none_po_kernel(
                 in_=w_bf[:, 2 * a : 2 * a + 2, :, :].rearrange("p t m j -> p (t m j)"),
             )
 
-        res_whole, res_last = res_late
         res_sb = {}
         for t in range(2):
             res_sb[0, 2 + t], res_sb[1, 2 + t] = res_early[:, t, :], res_last[:, t, :]
@@ -170,7 +177,7 @@ def tile_picked_phout_none_po_kernel(
             )
 
         codes = [
-            shared.tile([P, HALF], I32, name="y_codes0", offset=2 * T, align_bytes=64),
+            shared.tile([P, HALF], I32, name="y_codes0", offset=0, align_bytes=64),
             sb.tile([P, HALF], I32, name="y_codes1", align_bytes=64),
         ]
         quantise_y(first_half[:], codes[0][:], 0, HALF)

@@ -23,6 +23,7 @@ W_FIRST = 1024
 SCALAR_W = 64
 GPSIMD_Y = 72
 VECTOR_Y = 160
+PIECE = 2 * HALF * 4
 
 
 def tile_picked_phout_none_po_kernel(
@@ -38,7 +39,7 @@ def tile_picked_phout_none_po_kernel(
         nc.vector.memset(scale_table[:].bitcast(I32), 0)
 
         w_rows = w1.rearrange("(p j) n -> p (j n)", j=PACK)
-        w_raw = shared.tile([P, PACK * N], F32, name="w_raw", offset=T, align_bytes=64)
+        w_raw = shared.tile([P, PACK * N], F32, name="w_raw", offset=2 * PIECE, align_bytes=64)
         nc.sync.dma_start(w_raw[:, 0:W_FIRST], w_rows[:, 0:W_FIRST])
         offsets = sb.tile([P, S // 16], U16, name="offsets")
         nc.sync.dma_start(offsets[:], offs)
@@ -51,31 +52,25 @@ def tile_picked_phout_none_po_kernel(
         nc.sync.dma_start(word_table[:], x_words[0].rearrange("p c r -> p (c r)").bitcast(I32))
 
         res_rows = res.rearrange("(p t) s -> p t s", t=PACK)
-        res_early = sb.tile([P, 2, HALF], F32, name="res_sb00", align_bytes=64)
-        nc.sync.dma_start(res_early[:], res_rows[:, 2:4, 0:HALF])
+        res_sb = {}
 
-        res_whole = sb.tile([P, 2, S], F32, name="res_whole", align_bytes=64)
-        nc.sync.dma_start(res_whole[:], res_rows[:, 0:2, :])
-        res_last = shared.tile([P, 2, HALF], F32, name="res_last", offset=0, align_bytes=64)
-        nc.sync.dma_start(res_last[:], res_rows[:, 2:4, HALF:S])
+        def load_residual(piece, c, t):
+            nc.sync.dma_start(piece[:], res_rows[:, t : t + 2, c * HALF : (c + 1) * HALF])
+            res_sb[c, t], res_sb[c, t + 1] = piece[:, 0, :], piece[:, 1, :]
+
+        load_residual(sb.tile([P, 2, HALF], F32, name="res00", align_bytes=64), 0, 0)
 
         gate_sb = sb.tile([P, PACK], F32, name="gate_sb")
         nc.gpsimd.dma_start(gate_sb[:], gate.rearrange("(p t) o -> p (t o)", t=PACK))
 
-        picked = []
-        for c in range(2):
-            piece = sb.tile([P, HALF], U8, name="picked_scales%d" % c, align_bytes=64)
-            cols = slice(c * HALF // 16, (c + 1) * HALF // 16)
-            nc.vector.tensor_copy(piece[:], scale_table[:].indirect(offsets[:, cols]))
-            picked.append(piece)
-
-        def place_rows(plane, rows):
-            nc.vector.tensor_copy(plane[:].bitcast(I32), rows[:].bitcast(I32))
-            for e in range(2):
-                nc.scalar.dma_start(plane[:].bitcast(I32)[2 + e : P : 32, :], plane[:].bitcast(I32)[16 + e : P : 32, :])
-
-        plane_first = sb.tile([P, HALF], U8, name="x_plane0", align_bytes=64)
-        place_rows(plane_first, picked[0])
+        picked = shared.tile([P, S], U8, name="picked_scales", offset=PIECE - HALF, align_bytes=64)
+        nc.vector.tensor_copy(picked[:], scale_table[:].indirect(offsets[:]))
+        x_plane = sb.tile([P, S], U8, name="x_plane", align_bytes=64)
+        nc.vector.tensor_copy(x_plane[:].bitcast(I32), picked[:].bitcast(I32))
+        for e in range(2):
+            nc.sync.dma_start(x_plane[:].bitcast(I32)[2 + e : P : 32, :], x_plane[:].bitcast(I32)[16 + e : P : 32, :])
+        load_residual(shared.tile([P, 2, HALF], F32, name="res02", offset=0, align_bytes=64), 0, 2)
+        load_residual(shared.tile([P, 2, HALF], F32, name="res10", offset=PIECE, align_bytes=64), 1, 0)
 
         w_bf = sb.tile([P, PACK, P, PACK], BF16, name="w_bf", align_bytes=64)
 
@@ -91,9 +86,7 @@ def tile_picked_phout_none_po_kernel(
                 w_view[:, :, SCALAR_W:P, 2 * a : 2 * a + 2].rearrange("p j m b -> p m j b"),
             )
 
-        plane_second = shared.tile([P, HALF], U8, name="x_plane1", offset=T, align_bytes=64)
-        place_rows(plane_second, picked[1])
-        x_plane = [plane_first, plane_second]
+        load_residual(shared.tile([P, 2, HALF], F32, name="res12", offset=2 * PIECE, align_bytes=64), 1, 2)
 
         w_codes = sb.tile([P, N], U32, name="w_codes", align_bytes=64)
         w_plane = sb.tile([P, N], U8, name="w_plane", align_bytes=64)
@@ -104,11 +97,6 @@ def tile_picked_phout_none_po_kernel(
                 scales=w_plane[:, cols],
                 in_=w_bf[:, 2 * a : 2 * a + 2, :, :].rearrange("p t m j -> p (t m j)"),
             )
-
-        res_sb = {}
-        for t in range(2):
-            res_sb[0, 2 + t], res_sb[1, 2 + t] = res_early[:, t, :], res_last[:, t, :]
-            res_sb[0, t], res_sb[1, t] = res_whole[:, t, 0:HALF], res_whole[:, t, HALF:S]
 
         picked_words = []
         for c in range(2):
@@ -123,14 +111,14 @@ def tile_picked_phout_none_po_kernel(
         y = [sb.tile([P, PACK, HALF], F32, name="y%d" % c, align_bytes=64) for c in range(2)]
         acc = {}
         for c in range(2):
-            for t in (2, 3, 0, 1) if c == 0 else range(PACK):
+            for t in range(PACK):
                 acc[c, t] = ps.tile([P, HALF], F32, name="acc%d%d" % (c, t))
                 nc.tensor.matmul_mx(
                     out=acc[c, t][:],
                     lhsT=w_codes[:, t * P : (t + 1) * P].bitcast(FP8X4),
                     lhsT_scale=w_plane[:, t * P : (t + 1) * P],
                     rhs=picked_words[c][:].bitcast(FP8X4),
-                    rhs_scale=x_plane[c][:],
+                    rhs_scale=x_plane[:, c * HALF : (c + 1) * HALF],
                     start=True,
                     stop=True,
                 )
@@ -143,13 +131,12 @@ def tile_picked_phout_none_po_kernel(
         def store_y(c, t, rows):
             nc.sync.dma_start(out_rows[:, t : t + rows, c * HALF : (c + 1) * HALF], y[c][:, t : t + rows, :])
 
-        for t in (2, 3):
+        for t in range(PACK):
             finish(0, t, 0, HALF)
             store_y(0, t, 1)
-        for c in range(2):
-            finish(c, 0, 0, HALF)
-            finish(c, 1, 0, HALF)
-            store_y(c, 0, 2)
+        finish(1, 0, 0, HALF)
+        finish(1, 1, 0, HALF)
+        store_y(1, 0, 2)
         finish(1, 2, 0, HALF)
         finish(1, 3, 0, VECTOR_Y)
         finish(1, 3, VECTOR_Y, HALF)
@@ -177,7 +164,7 @@ def tile_picked_phout_none_po_kernel(
             )
 
         codes = [
-            shared.tile([P, HALF], I32, name="y_codes0", offset=0, align_bytes=64),
+            shared.tile([P, HALF], I32, name="y_codes0", offset=2 * PIECE, align_bytes=64),
             sb.tile([P, HALF], I32, name="y_codes1", align_bytes=64),
         ]
         quantise_y(first_half[:], codes[0][:], 0, HALF)

@@ -61,7 +61,7 @@ def tile_picked_phout_none_po_kernel(
         load_residual(sb.tile([P, 2, HALF], F32, name="res00", align_bytes=64), 0, 0)
 
         gate_sb = sb.tile([P, PACK], F32, name="gate_sb")
-        nc.gpsimd.dma_start(gate_sb[:], gate.rearrange("(p t) o -> p (t o)", t=PACK))
+        nc.sync.dma_start(gate_sb[:], gate.rearrange("(p t) o -> p (t o)", t=PACK))
 
         picked = shared.tile([P, S], U8, name="picked_scales", offset=PIECE - HALF, align_bytes=64)
         nc.vector.tensor_copy(picked[:], scale_table[:].indirect(offsets[:]))
@@ -131,12 +131,13 @@ def tile_picked_phout_none_po_kernel(
         def store_y(c, t, rows):
             nc.sync.dma_start(out_rows[:, t : t + rows, c * HALF : (c + 1) * HALF], y[c][:, t : t + rows, :])
 
-        for t in range(PACK):
+        for t in range(2):
             finish(0, t, 0, HALF)
             store_y(0, t, 1)
-        finish(1, 0, 0, HALF)
-        finish(1, 1, 0, HALF)
-        store_y(1, 0, 2)
+        for c, t in ((0, 2), (1, 0)):
+            finish(c, t, 0, HALF)
+            finish(c, t + 1, 0, HALF)
+            store_y(c, t, 2)
         finish(1, 2, 0, HALF)
         finish(1, 3, 0, VECTOR_Y)
         finish(1, 3, VECTOR_Y, HALF)

@@ -39,7 +39,7 @@ def tile_picked_phout_none_po_kernel(
         nc.vector.memset(scale_table[:].bitcast(I32), 0)
 
         w_rows = w1.rearrange("(p j) n -> p (j n)", j=PACK)
-        w_raw = shared.tile([P, PACK * N], F32, name="w_raw", offset=2 * PIECE, align_bytes=64)
+        w_raw = shared.tile([P, PACK * N], F32, name="w_raw", offset=2 * PIECE + 64, align_bytes=64)
         nc.sync.dma_start(w_raw[:, 0:W_FIRST], w_rows[:, 0:W_FIRST])
         offsets = sb.tile([P, S // 16], U16, name="offsets")
         nc.sync.dma_start(offsets[:], offs)
@@ -60,8 +60,6 @@ def tile_picked_phout_none_po_kernel(
 
         load_residual(sb.tile([P, 2, HALF], F32, name="res00", align_bytes=64), 0, 0)
 
-        gate_sb = sb.tile([P, PACK], F32, name="gate_sb")
-        nc.sync.dma_start(gate_sb[:], gate.rearrange("(p t) o -> p (t o)", t=PACK))
 
         picked = shared.tile([P, S], U8, name="picked_scales", offset=PIECE - HALF, align_bytes=64)
         nc.vector.tensor_copy(picked[:], scale_table[:].indirect(offsets[:]))
@@ -69,8 +67,10 @@ def tile_picked_phout_none_po_kernel(
         nc.vector.tensor_copy(x_plane[:].bitcast(I32), picked[:].bitcast(I32))
         for e in range(2):
             nc.sync.dma_start(x_plane[:].bitcast(I32)[2 + e : P : 32, :], x_plane[:].bitcast(I32)[16 + e : P : 32, :])
+        gate_sb = shared.tile([P, PACK], F32, name="gate_sb", offset=PIECE, align_bytes=64)
+        nc.sync.dma_start(gate_sb[:], gate.rearrange("(p t) o -> p (t o)", t=PACK))
         load_residual(shared.tile([P, 2, HALF], F32, name="res02", offset=0, align_bytes=64), 0, 2)
-        load_residual(shared.tile([P, 2, HALF], F32, name="res10", offset=PIECE, align_bytes=64), 1, 0)
+        load_residual(shared.tile([P, 2, HALF], F32, name="res10", offset=PIECE + 64, align_bytes=64), 1, 0)
 
         w_bf = sb.tile([P, PACK, P, PACK], BF16, name="w_bf", align_bytes=64)
 
@@ -86,7 +86,7 @@ def tile_picked_phout_none_po_kernel(
                 w_view[:, :, SCALAR_W:P, 2 * a : 2 * a + 2].rearrange("p j m b -> p m j b"),
             )
 
-        load_residual(shared.tile([P, 2, HALF], F32, name="res12", offset=2 * PIECE, align_bytes=64), 1, 2)
+        load_residual(shared.tile([P, 2, HALF], F32, name="res12", offset=2 * PIECE + 64, align_bytes=64), 1, 2)
 
         w_codes = sb.tile([P, N], U32, name="w_codes", align_bytes=64)
         w_plane = sb.tile([P, N], U8, name="w_plane", align_bytes=64)
@@ -165,7 +165,7 @@ def tile_picked_phout_none_po_kernel(
             )
 
         codes = [
-            shared.tile([P, HALF], I32, name="y_codes0", offset=2 * PIECE, align_bytes=64),
+            shared.tile([P, HALF], I32, name="y_codes0", offset=2 * PIECE + 64, align_bytes=64),
             sb.tile([P, HALF], I32, name="y_codes1", align_bytes=64),
         ]
         quantise_y(first_half[:], codes[0][:], 0, HALF)

@@ -43,9 +43,7 @@ def tile_picked_phout_none_po_kernel(
         nc.sync.dma_start(w_raw[:, 0:W_FIRST], w_rows[:, 0:W_FIRST])
         offsets = sb.tile([P, S // 16], U16, name="offsets")
         nc.sync.dma_start(offsets[:], offs)
-        scale_rows = x_scales[0].bitcast(I32).rearrange("(u e) c -> e u c", e=2)
-        for e in range(2):
-            nc.sync.dma_start(scale_table[:].bitcast(I32)[e:P:16, :], scale_rows[e])
+        nc.sync.dma_start(scale_table[:].bitcast(I32)[0:P:8, :], x_scales[0].bitcast(I32))
         nc.sync.dma_start(w_raw[:, W_FIRST : PACK * N], w_rows[:, W_FIRST : PACK * N])
 
         word_table = sb.tile([P, T], I32, name="word_table", align_bytes=64)
@@ -65,8 +63,8 @@ def tile_picked_phout_none_po_kernel(
         nc.vector.tensor_copy(picked[:], scale_table[:].indirect(offsets[:]))
         x_plane = sb.tile([P, S], U8, name="x_plane", align_bytes=64)
         nc.vector.tensor_copy(x_plane[:].bitcast(I32), picked[:].bitcast(I32))
-        for e in range(2):
-            nc.sync.dma_start(x_plane[:].bitcast(I32)[2 + e : P : 32, :], x_plane[:].bitcast(I32)[16 + e : P : 32, :])
+        for r in range(1, 4):
+            nc.sync.dma_start(x_plane[:].bitcast(I32)[r:P:32, :], x_plane[:].bitcast(I32)[8 * r : P : 32, :])
         gate_sb = shared.tile([P, PACK], F32, name="gate_sb", offset=PIECE, align_bytes=64)
         nc.sync.dma_start(gate_sb[:], gate.rearrange("(p t) o -> p (t o)", t=PACK))
         load_residual(shared.tile([P, 2, HALF], F32, name="res02", offset=0, align_bytes=64), 0, 2)

@@ -24,6 +24,7 @@ SCALAR_W = 64
 GPSIMD_Y = 72
 VECTOR_Y = 160
 PIECE = 2 * HALF * 4
+LINE = 256
 
 
 def tile_picked_phout_none_po_kernel(
@@ -35,18 +36,18 @@ def tile_picked_phout_none_po_kernel(
         shared = ctx.enter_context(tc.tile_pool(name="shared", bufs=1))
         ps = ctx.enter_context(tc.psum_pool(name="ps", bufs=1))
 
-        scale_table = sb.tile([P, T], U8, name="scale_table", align_bytes=64)
+        scale_table = sb.tile([P, T], U8, name="scale_table", align_bytes=LINE)
         nc.vector.memset(scale_table[:].bitcast(I32), 0)
 
         w_rows = w1.rearrange("(p j) n -> p (j n)", j=PACK)
-        w_raw = shared.tile([P, PACK * N], F32, name="w_raw", offset=2 * PIECE + 64, align_bytes=64)
+        w_raw = shared.tile([P, PACK * N], F32, name="w_raw", offset=2 * PIECE + LINE, align_bytes=LINE)
         nc.sync.dma_start(w_raw[:, 0:W_FIRST], w_rows[:, 0:W_FIRST])
-        offsets = sb.tile([P, S // 16], U16, name="offsets")
+        offsets = sb.tile([P, S // 16], U16, name="offsets", align_bytes=LINE)
         nc.sync.dma_start(offsets[:], offs)
         nc.sync.dma_start(scale_table[:].bitcast(I32)[0:P:8, :], x_scales[0].bitcast(I32))
         nc.sync.dma_start(w_raw[:, W_FIRST : PACK * N], w_rows[:, W_FIRST : PACK * N])
 
-        word_table = sb.tile([P, T], I32, name="word_table", align_bytes=64)
+        word_table = sb.tile([P, T], I32, name="word_table", align_bytes=LINE)
         nc.sync.dma_start(word_table[:], x_words[0].rearrange("p c r -> p (c r)").bitcast(I32))
 
         res_rows = res.rearrange("(p t) s -> p t s", t=PACK)
@@ -56,21 +57,21 @@ def tile_picked_phout_none_po_kernel(
             nc.sync.dma_start(piece[:], res_rows[:, t : t + 2, c * HALF : (c + 1) * HALF])
             res_sb[c, t], res_sb[c, t + 1] = piece[:, 0, :], piece[:, 1, :]
 
-        load_residual(sb.tile([P, 2, HALF], F32, name="res00", align_bytes=64), 0, 0)
+        load_residual(sb.tile([P, 2, HALF], F32, name="res00", align_bytes=LINE), 0, 0)
 
 
-        picked = shared.tile([P, S], U8, name="picked_scales", offset=PIECE - HALF, align_bytes=64)
+        picked = shared.tile([P, S], U8, name="picked_scales", offset=PIECE - LINE // 2, align_bytes=64)
         nc.vector.tensor_copy(picked[:], scale_table[:].indirect(offsets[:]))
-        x_plane = sb.tile([P, S], U8, name="x_plane", align_bytes=64)
+        x_plane = sb.tile([P, S], U8, name="x_plane", align_bytes=LINE)
         nc.vector.tensor_copy(x_plane[:].bitcast(I32), picked[:].bitcast(I32))
         for r in range(1, 4):
             nc.sync.dma_start(x_plane[:].bitcast(I32)[r:P:32, :], x_plane[:].bitcast(I32)[8 * r : P : 32, :])
-        gate_sb = shared.tile([P, PACK], F32, name="gate_sb", offset=PIECE, align_bytes=64)
+        gate_sb = shared.tile([P, PACK], F32, name="gate_sb", offset=PIECE, align_bytes=LINE)
         nc.sync.dma_start(gate_sb[:], gate.rearrange("(p t) o -> p (t o)", t=PACK))
-        load_residual(shared.tile([P, 2, HALF], F32, name="res02", offset=0, align_bytes=64), 0, 2)
-        load_residual(shared.tile([P, 2, HALF], F32, name="res10", offset=PIECE + 64, align_bytes=64), 1, 0)
+        load_residual(shared.tile([P, 2, HALF], F32, name="res02", offset=0, align_bytes=LINE), 0, 2)
+        load_residual(shared.tile([P, 2, HALF], F32, name="res10", offset=PIECE + LINE, align_bytes=LINE), 1, 0)
 
-        w_bf = sb.tile([P, PACK, P, PACK], BF16, name="w_bf", align_bytes=64)
+        w_bf = sb.tile([P, PACK, P, PACK], BF16, name="w_bf", align_bytes=LINE)
 
         w_view = w_raw[:].rearrange("p (j m t) -> p j m t", j=PACK, t=PACK)
         for u, tiles in ((0, slice(0, 4)), (1, slice(0, 2)), (1, slice(2, 4))):
@@ -84,10 +85,10 @@ def tile_picked_phout_none_po_kernel(
                 w_view[:, :, SCALAR_W:P, 2 * a : 2 * a + 2].rearrange("p j m b -> p m j b"),
             )
 
-        load_residual(shared.tile([P, 2, HALF], F32, name="res12", offset=2 * PIECE + 64, align_bytes=64), 1, 2)
+        load_residual(shared.tile([P, 2, HALF], F32, name="res12", offset=2 * PIECE + LINE, align_bytes=LINE), 1, 2)
 
-        w_codes = sb.tile([P, N], U32, name="w_codes", align_bytes=64)
-        w_plane = sb.tile([P, N], U8, name="w_plane", align_bytes=64)
+        w_codes = sb.tile([P, N], U32, name="w_codes", align_bytes=LINE)
+        w_plane = sb.tile([P, N], U8, name="w_plane", align_bytes=LINE)
         for a in range(2):
             cols = slice(a * 2 * P, (a + 1) * 2 * P)
             nc.vector.quantize_mx(
@@ -98,15 +99,15 @@ def tile_picked_phout_none_po_kernel(
 
         picked_words = []
         for c in range(2):
-            piece = sb.tile([P, HALF], U32, name="picked_words%d" % c, align_bytes=64)
+            piece = sb.tile([P, HALF], U32, name="picked_words%d" % c, align_bytes=LINE)
             cols = slice(c * HALF // 16, (c + 1) * HALF // 16)
             nc.vector.tensor_copy(piece[:], word_table[:].bitcast(U32).indirect(offsets[:, cols]))
             picked_words.append(piece)
 
         out_rows = out_0.rearrange("(p t) s -> p t s", t=PACK)
         out_words = out_1[0].rearrange("p c r -> p (c r)").bitcast(I32)
-        y_plane = sb.tile([P, S], U8, name="y_plane", align_bytes=64)
-        y = [sb.tile([P, PACK, HALF], F32, name="y%d" % c, align_bytes=64) for c in range(2)]
+        y_plane = sb.tile([P, S], U8, name="y_plane", align_bytes=LINE)
+        y = [sb.tile([P, PACK, HALF], F32, name="y%d" % c, align_bytes=LINE) for c in range(2)]
         acc = {}
         for c in range(2):
             for t in range(PACK):
@@ -146,7 +147,7 @@ def tile_picked_phout_none_po_kernel(
                 out=codes.bitcast(FP8X4), scales=y_plane[:, lo:hi], in_=rounded.rearrange("p s t -> p (s t)")
             )
 
-        first_half = sb.tile([P, HALF, PACK], BF16, name="first_half", align_bytes=64)
+        first_half = sb.tile([P, HALF, PACK], BF16, name="first_half", align_bytes=LINE)
         split = HALF - GPSIMD_Y
         nc.scalar.copy(
             first_half[:, 0:split, :].rearrange("p (s i) t -> p s t i", i=2),
@@ -155,7 +156,7 @@ def tile_picked_phout_none_po_kernel(
         nc.gpsimd.tensor_scalar(
             first_half[:, split:HALF, :], y[0][:, :, split:HALF].rearrange("p t s -> p s t"), 1.0, 0.0, MULT, ADD
         )
-        second_half = sb.tile([P, HALF, PACK], BF16, name="second_half", align_bytes=64)
+        second_half = sb.tile([P, HALF, PACK], BF16, name="second_half", align_bytes=LINE)
         for engine_copy, lo, hi in ((nc.vector.tensor_copy, 0, VECTOR_Y), (nc.scalar.copy, VECTOR_Y, HALF)):
             engine_copy(
                 second_half[:, lo:hi, :].rearrange("p (s i) t -> p s t i", i=2),
@@ -163,8 +164,8 @@ def tile_picked_phout_none_po_kernel(
             )
 
         codes = [
-            shared.tile([P, HALF], I32, name="y_codes0", offset=2 * PIECE + 64, align_bytes=64),
-            sb.tile([P, HALF], I32, name="y_codes1", align_bytes=64),
+            shared.tile([P, HALF], I32, name="y_codes0", offset=2 * PIECE + LINE, align_bytes=LINE),
+            sb.tile([P, HALF], I32, name="y_codes1", align_bytes=LINE),
         ]
         quantise_y(first_half[:], codes[0][:], 0, HALF)
         nc.sync.dma_start(out_words[:, 0:HALF], codes[0][:])

@@ -109,29 +109,38 @@ def tile_picked_phout_none_po_kernel(
         y_plane = sb.tile([P, S], U8, name="y_plane", align_bytes=LINE)
         y = [sb.tile([P, PACK, HALF], F32, name="y%d" % c, align_bytes=LINE) for c in range(2)]
         acc = {}
+
+        def multiply(bank, c, t, lo, hi):
+            nc.tensor.matmul_mx(
+                out=bank[:, lo:hi],
+                lhsT=w_codes[:, t * P : (t + 1) * P].bitcast(FP8X4),
+                lhsT_scale=w_plane[:, t * P : (t + 1) * P],
+                rhs=picked_words[c][:, lo:hi].bitcast(FP8X4),
+                rhs_scale=x_plane[:, c * HALF + lo : c * HALF + hi],
+                start=True,
+                stop=True,
+            )
+
+        def finish(c, t, lo, hi, bank=None):
+            source = acc[c, t] if bank is None else bank
+            nc.vector.scalar_tensor_tensor(
+                y[c][:, t, lo:hi], source[:, lo:hi], gate_sb[:, t : t + 1], res_sb[c, t][:, lo:hi], MULT, ADD
+            )
+
+        first_bank = ps.tile([P, HALF], F32, name="first_bank", tag="last_bank")
+        multiply(first_bank, 0, 0, 0, QUARTER)
+        finish(0, 0, 0, QUARTER, first_bank)
         for c in range(2):
             for t in range(PACK):
-                acc[c, t] = ps.tile([P, HALF], F32, name="acc%d%d" % (c, t))
-                nc.tensor.matmul_mx(
-                    out=acc[c, t][:],
-                    lhsT=w_codes[:, t * P : (t + 1) * P].bitcast(FP8X4),
-                    lhsT_scale=w_plane[:, t * P : (t + 1) * P],
-                    rhs=picked_words[c][:].bitcast(FP8X4),
-                    rhs_scale=x_plane[:, c * HALF : (c + 1) * HALF],
-                    start=True,
-                    stop=True,
-                )
-
-        def finish(c, t, lo, hi):
-            nc.vector.scalar_tensor_tensor(
-                y[c][:, t, lo:hi], acc[c, t][:, lo:hi], gate_sb[:, t : t + 1], res_sb[c, t][:, lo:hi], MULT, ADD
-            )
+                tag = "last_bank" if (c, t) == (1, PACK - 1) else "acc%d%d" % (c, t)
+                acc[c, t] = ps.tile([P, HALF], F32, name="acc%d%d" % (c, t), tag=tag)
+                multiply(acc[c, t], c, t, QUARTER if (c, t) == (0, 0) else 0, HALF)
 
         def store_y(c, t, rows):
             nc.sync.dma_start(out_rows[:, t : t + rows, c * HALF : (c + 1) * HALF], y[c][:, t : t + rows, :])
 
         for t in range(2):
-            finish(0, t, 0, HALF)
+            finish(0, t, QUARTER if t == 0 else 0, HALF)
             store_y(0, t, 1)
         for c, t in ((0, 2), (1, 0)):
             finish(c, t, 0, HALF)

@@ -20,7 +20,6 @@ PACK = 4
 HALF = S // 2
 QUARTER = S // 4
 W_FIRST = 1024
-SCALAR_W = 64
 GPSIMD_Y = 72
 VECTOR_Y = 160
 PIECE = 2 * HALF * 4
@@ -64,8 +63,12 @@ def tile_picked_phout_none_po_kernel(
         nc.vector.tensor_copy(picked[:], scale_table[:].indirect(offsets[:]))
         x_plane = sb.tile([P, S], U8, name="x_plane", align_bytes=LINE)
         nc.vector.tensor_copy(x_plane[:].bitcast(I32), picked[:].bitcast(I32))
-        for r in range(1, 4):
-            nc.sync.dma_start(x_plane[:].bitcast(I32)[r:P:32, :], x_plane[:].bitcast(I32)[8 * r : P : 32, :])
+
+        def move_rows(queue, r):
+            queue.dma_start(x_plane[:].bitcast(I32)[r:P:32, :], x_plane[:].bitcast(I32)[8 * r : P : 32, :])
+
+        for r in range(1, 3):
+            move_rows(nc.sync, r)
         gate_sb = shared.tile([P, PACK], F32, name="gate_sb", offset=PIECE, align_bytes=LINE)
         nc.sync.dma_start(gate_sb[:], gate.rearrange("(p t) o -> p (t o)", t=PACK))
         load_residual(shared.tile([P, 2, HALF], F32, name="res02", offset=0, align_bytes=LINE), 0, 2)
@@ -74,15 +77,15 @@ def tile_picked_phout_none_po_kernel(
         w_bf = sb.tile([P, PACK, P, PACK], BF16, name="w_bf", align_bytes=LINE)
 
         w_view = w_raw[:].rearrange("p (j m t) -> p j m t", j=PACK, t=PACK)
-        for u, tiles in ((0, slice(0, 4)), (1, slice(0, 2)), (1, slice(2, 4))):
-            nc.scalar.copy(
-                w_bf[:, tiles, 0:SCALAR_W, 2 * u : 2 * u + 2].rearrange("p t (g i) j -> p g t i j", i=2),
-                w_view[:, 2 * u : 2 * u + 2, 0:SCALAR_W, tiles].rearrange("p j (g i) t -> p g t i j", i=2),
-            )
+        nc.scalar.copy(
+            w_bf[:, :, :, 0:2].rearrange("p t (g i) j -> p g t i j", i=2),
+            w_view[:, 0:2, :, :].rearrange("p j (g i) t -> p g t i j", i=2),
+        )
+        move_rows(nc.scalar, 3)
         for a in range(2):
             nc.vector.tensor_copy(
-                w_bf[:, 2 * a : 2 * a + 2, SCALAR_W:P, :].rearrange("p b m j -> p m j b"),
-                w_view[:, :, SCALAR_W:P, 2 * a : 2 * a + 2].rearrange("p j m b -> p m j b"),
+                w_bf[:, 2 * a : 2 * a + 2, :, 2:4].rearrange("p t (g i) j -> p g t i j", i=2),
+                w_view[:, 2:4, :, 2 * a : 2 * a + 2].rearrange("p j (g i) t -> p g t i j", i=2),
             )
 
         load_residual(shared.tile([P, 2, HALF], F32, name="res12", offset=2 * PIECE + LINE, align_bytes=LINE), 1, 2)

from contextlib import ExitStack

import concourse.mybir as mybir

K, T, S, N = 512, 2048, 512, 512
FLOPS = 2 * K * N * S

F32 = mybir.dt.float32
BF16 = mybir.dt.bfloat16
I32 = mybir.dt.int32
U32 = mybir.dt.uint32
U16 = mybir.dt.uint16
U8 = mybir.dt.uint8
FP8X4 = mybir.dt.float8_e4m3fn_x4
MULT = mybir.AluOpType.mult
ADD = mybir.AluOpType.add

P = 128
PACK = 4
HALF = S // 2
QUARTER = S // 4
W_FIRST = 1024
GPSIMD_Y = 72
VECTOR_Y = 160
PIECE = 2 * HALF * 4
LINE = 256


def tile_picked_phout_none_po_kernel(
    tc, x_words, x_scales, w1, res, gate, offs, out_0, out_1, out_2
):
    nc = tc.nc
    with ExitStack() as ctx:
        sb = ctx.enter_context(tc.tile_pool(name="sb", bufs=1))
        shared = ctx.enter_context(tc.tile_pool(name="shared", bufs=1))
        ps = ctx.enter_context(tc.psum_pool(name="ps", bufs=1))

        scale_table = sb.tile([P, T], U8, name="scale_table", align_bytes=LINE)
        nc.vector.memset(scale_table[:].bitcast(I32), 0)

        w_rows = w1.rearrange("(p j) n -> p (j n)", j=PACK)
        w_raw = shared.tile([P, PACK * N], F32, name="w_raw", offset=2 * PIECE + LINE, align_bytes=LINE)
        nc.sync.dma_start(w_raw[:, 0:W_FIRST], w_rows[:, 0:W_FIRST])
        offsets = sb.tile([P, S // 16], U16, name="offsets", align_bytes=LINE)
        nc.sync.dma_start(offsets[:], offs)
        nc.sync.dma_start(scale_table[:].bitcast(I32)[0:P:8, :], x_scales[0].bitcast(I32))
        nc.sync.dma_start(w_raw[:, W_FIRST : PACK * N], w_rows[:, W_FIRST : PACK * N])

        word_table = sb.tile([P, T], I32, name="word_table", align_bytes=LINE)
        nc.sync.dma_start(word_table[:], x_words[0].rearrange("p c r -> p (c r)").bitcast(I32))

        res_rows = res.rearrange("(p t) s -> p t s", t=PACK)
        res_sb = {}

        def load_residual(piece, c, t):
            nc.sync.dma_start(piece[:], res_rows[:, t : t + 2, c * HALF : (c + 1) * HALF])
            res_sb[c, t], res_sb[c, t + 1] = piece[:, 0, :], piece[:, 1, :]

        load_residual(sb.tile([P, 2, HALF], F32, name="res00", align_bytes=LINE), 0, 0)


        picked = shared.tile([P, S], U8, name="picked_scales", offset=PIECE - LINE // 2, align_bytes=64)
        nc.vector.tensor_copy(picked[:], scale_table[:].indirect(offsets[:]))
        x_plane = sb.tile([P, S], U8, name="x_plane", align_bytes=LINE)
        nc.vector.tensor_copy(x_plane[:].bitcast(I32), picked[:].bitcast(I32))

        def move_rows(queue, r):
            queue.dma_start(x_plane[:].bitcast(I32)[r:P:32, :], x_plane[:].bitcast(I32)[8 * r : P : 32, :])

        for r in range(1, 3):
            move_rows(nc.sync, r)
        gate_sb = shared.tile([P, PACK], F32, name="gate_sb", offset=PIECE, align_bytes=LINE)
        nc.sync.dma_start(gate_sb[:], gate.rearrange("(p t) o -> p (t o)", t=PACK))
        load_residual(shared.tile([P, 2, HALF], F32, name="res02", offset=0, align_bytes=LINE), 0, 2)
        load_residual(shared.tile([P, 2, HALF], F32, name="res10", offset=PIECE + LINE, align_bytes=LINE), 1, 0)

        w_bf = sb.tile([P, PACK, P, PACK], BF16, name="w_bf", align_bytes=LINE)

        w_view = w_raw[:].rearrange("p (j m t) -> p j m t", j=PACK, t=PACK)
        nc.scalar.copy(
            w_bf[:, :, :, 0:2].rearrange("p t (g i) j -> p g t i j", i=2),
            w_view[:, 0:2, :, :].rearrange("p j (g i) t -> p g t i j", i=2),
        )
        move_rows(nc.scalar, 3)
        for a in range(2):
            nc.vector.tensor_copy(
                w_bf[:, 2 * a : 2 * a + 2, :, 2:4].rearrange("p t (g i) j -> p g t i j", i=2),
                w_view[:, 2:4, :, 2 * a : 2 * a + 2].rearrange("p j (g i) t -> p g t i j", i=2),
            )

        load_residual(shared.tile([P, 2, HALF], F32, name="res12", offset=2 * PIECE + LINE, align_bytes=LINE), 1, 2)

        w_codes = sb.tile([P, N], U32, name="w_codes", align_bytes=LINE)
        w_plane = sb.tile([P, N], U8, name="w_plane", align_bytes=LINE)
        for a in range(2):
            cols = slice(a * 2 * P, (a + 1) * 2 * P)
            nc.vector.quantize_mx(
                out=w_codes[:, cols].bitcast(FP8X4),
                scales=w_plane[:, cols],
                in_=w_bf[:, 2 * a : 2 * a + 2, :, :].rearrange("p t m j -> p (t m j)"),
            )

        picked_words = []
        for c in range(2):
            piece = sb.tile([P, HALF], U32, name="picked_words%d" % c, align_bytes=LINE)
            cols = slice(c * HALF // 16, (c + 1) * HALF // 16)
            nc.vector.tensor_copy(piece[:], word_table[:].bitcast(U32).indirect(offsets[:, cols]))
            picked_words.append(piece)

        out_rows = out_0.rearrange("(p t) s -> p t s", t=PACK)
        out_words = out_1[0].rearrange("p c r -> p (c r)").bitcast(I32)
        y_plane = sb.tile([P, S], U8, name="y_plane", align_bytes=LINE)
        y = [sb.tile([P, PACK, HALF], F32, name="y%d" % c, align_bytes=LINE) for c in range(2)]
        acc = {}

        def multiply(bank, c, t, lo, hi):
            nc.tensor.matmul_mx(
                out=bank[:, lo:hi],
                lhsT=w_codes[:, t * P : (t + 1) * P].bitcast(FP8X4),
                lhsT_scale=w_plane[:, t * P : (t + 1) * P],
                rhs=picked_words[c][:, lo:hi].bitcast(FP8X4),
                rhs_scale=x_plane[:, c * HALF + lo : c * HALF + hi],
                start=True,
                stop=True,
            )

        def finish(c, t, lo, hi, bank=None):
            source = acc[c, t] if bank is None else bank
            nc.vector.scalar_tensor_tensor(
                y[c][:, t, lo:hi], source[:, lo:hi], gate_sb[:, t : t + 1], res_sb[c, t][:, lo:hi], MULT, ADD
            )

        first_bank = ps.tile([P, HALF], F32, name="first_bank", tag="last_bank")
        multiply(first_bank, 0, 0, 0, QUARTER)
        finish(0, 0, 0, QUARTER, first_bank)
        for c in range(2):
            for t in range(PACK):
                tag = "last_bank" if (c, t) == (1, PACK - 1) else "acc%d%d" % (c, t)
                acc[c, t] = ps.tile([P, HALF], F32, name="acc%d%d" % (c, t), tag=tag)
                multiply(acc[c, t], c, t, QUARTER if (c, t) == (0, 0) else 0, HALF)

        def store_y(c, t, rows):
            nc.sync.dma_start(out_rows[:, t : t + rows, c * HALF : (c + 1) * HALF], y[c][:, t : t + rows, :])

        for t in range(2):
            finish(0, t, QUARTER if t == 0 else 0, HALF)
            store_y(0, t, 1)
        for c, t in ((0, 2), (1, 0)):
            finish(c, t, 0, HALF)
            finish(c, t + 1, 0, HALF)
            store_y(c, t, 2)
        finish(1, 2, 0, HALF)
        finish(1, 3, 0, VECTOR_Y)
        finish(1, 3, VECTOR_Y, HALF)
        store_y(1, 2, 2)

        def quantise_y(rounded, codes, lo, hi):
            nc.vector.quantize_mx(
                out=codes.bitcast(FP8X4), scales=y_plane[:, lo:hi], in_=rounded.rearrange("p s t -> p (s t)")
            )

        first_half = sb.tile([P, HALF, PACK], BF16, name="first_half", align_bytes=LINE)
        split = HALF - GPSIMD_Y
        nc.scalar.copy(
            first_half[:, 0:split, :].rearrange("p (s i) t -> p s t i", i=2),
            y[0][:, :, 0:split].rearrange("p t (s i) -> p s t i", i=2),
        )
        nc.gpsimd.tensor_scalar(
            first_half[:, split:HALF, :], y[0][:, :, split:HALF].rearrange("p t s -> p s t"), 1.0, 0.0, MULT, ADD
        )
        second_half = sb.tile([P, HALF, PACK], BF16, name="second_half", align_bytes=LINE)
        for engine_copy, lo, hi in ((nc.vector.tensor_copy, 0, VECTOR_Y), (nc.scalar.copy, VECTOR_Y, HALF)):
            engine_copy(
                second_half[:, lo:hi, :].rearrange("p (s i) t -> p s t i", i=2),
                y[1][:, :, lo:hi].rearrange("p t (s i) -> p s t i", i=2),
            )

        codes = [
            shared.tile([P, HALF], I32, name="y_codes0", offset=2 * PIECE + LINE, align_bytes=LINE),
            sb.tile([P, HALF], I32, name="y_codes1", align_bytes=LINE),
        ]
        quantise_y(first_half[:], codes[0][:], 0, HALF)
        nc.sync.dma_start(out_words[:, 0:HALF], codes[0][:])
        quantise_y(second_half[:, 0:QUARTER, :], codes[1][:, 0:QUARTER], HALF, S - QUARTER)
        quantise_y(second_half[:, QUARTER:HALF, :], codes[1][:, QUARTER:HALF], S - QUARTER, S)
        nc.sync.dma_start(out_words[:, HALF:S], codes[1][:])

        for q in range(4):
            queue = nc.scalar if q % 2 == 0 else nc.sync
            queue.dma_start(
                out_2[0].bitcast(I32)[4 * q : 4 * q + 4, :], y_plane[:].bitcast(I32)[32 * q : 32 * q + 4, :]
            )
